import numpy as np, ml_dtypes
CORES = [40,64,80,88,96,104,120,144]
N = 8
import mx_ref
BF = ml_dtypes.bfloat16
def tile(rs):
    return np.stack(rs, axis=2).reshape(128, -1).astype(BF)
def pick(q, e):
    c = np.concatenate([q[0].reshape(128, -1, 4), np.zeros((128, 1, 4), np.uint8)], axis=1); s = np.concatenate([q[1], np.ones((16, 1), np.uint8)], axis=1)
    return (np.ascontiguousarray(c[:, e].reshape(128, -1)), np.ascontiguousarray(s[:, e]))
def join(*qs):
    return (np.concatenate([q[0] for q in qs], axis=1), np.concatenate([q[1] for q in qs], axis=1))
def put(q, e, v):
    c, s = q[0].reshape(128, -1, 4).copy(), q[1].copy(); c[:, e] = v[0].reshape(128, -1, 4); s[:, e] = v[1]
    return (c.reshape(128, -1), s)
def pk(c, s):
    return (np.ascontiguousarray(c), mx_ref.live(s))
def emit(q):
    return q[0], q[1]
def packed(v, rng):
    q = [mx_ref.quantize(np.ascontiguousarray(v[r])) for r in range(N)]
    return np.stack([a for a, b in q]), np.stack([mx_ref.plane(b, rng) for a, b in q])
def values_of_codes():
    e, c = np.zeros((128, 128, 4), np.float32), np.zeros((128, 2, 4), np.uint8)
    e[np.arange(128), np.arange(128), 0] = 1
    c[:127, :, 0] = np.arange(256).reshape(2, 128).T[:127]
    return mx_ref.matmul(mx_ref.quantize(e.reshape(128, 512).astype(BF)), (c.reshape(128, 8), np.full((16, 2), 127, np.uint8))).T.reshape(-1).astype(np.float64)
CODE_VALUE, SCALE_VALUE = values_of_codes(), 2.0 ** (np.arange(256) - 127.0)
def decode(q):
    return (CODE_VALUE[q[0]].reshape(16, 8, -1, 4) * SCALE_VALUE[q[1]][:, None, :, None] + 0.0).reshape(128, -1).astype(np.float32)
def f(rng, *shape):
    return mx_ref.flush((rng.standard_normal(shape, dtype=np.float32) * np.exp2(rng.integers(-2, 3, shape[:-1] + (1,)))).astype(BF))
def wide(rng, *shape, cols=0):
    v = rng.standard_normal(shape, dtype=np.float32) * np.exp2(rng.integers(-12, 13, shape)).astype(np.float32)
    if cols: v *= np.repeat(np.exp2(rng.integers(-cols, cols + 1, shape[:-2] + (1, shape[-1] // 4))) * (rng.random(shape[:-2] + (1, shape[-1] // 4)) > 0.0625), 4, axis=-1).astype(np.float32)
    return mx_ref.flush(v.astype(BF))
C, H = 320, 128
DIST = [1, 2, 4]
def numbers_of(rng):
    return {"x": np.array(f(rng, N, 128, 4 * C)), "u": np.array(f(rng, N, 128, 512)), "v": np.array(f(rng, N, 128, 512))}
def changes(rng):
    return np.argsort(rng.random((N, 8, 8)), axis=2).astype(np.int32)
def layers(rng, still=[]):
    k = np.exp2(np.argsort(rng.random((N, 128, 1)), axis=1) % 5 - 6.0).astype(np.float32)
    w = np.array(mx_ref.flush((rng.standard_normal((N, 128, 2048), dtype=np.float32) * k).astype(BF))).reshape(N, 8, 16, 4, 8, 16, 4)
    for i in still:
        w[:, :, i] = 0
        w[:, :, :, :, :, i] = 0
    return w
def weights(rng, w):
    c, p = packed(np.ascontiguousarray(w).reshape(N, 128, 2048), rng)
    return {"wc": c, "ws": p}
def edges(rng, x):
    x = x.astype(np.float32).reshape(N, 8, 16, C, 4)
    k = (N, 8, 8, C, 4)
    a = (2 * rng.integers(64, 128, k) + 1) * np.exp2(-7.0 - rng.integers(8, 15, k)) * (rng.integers(0, 2, k) * 2.0 - 1.0)
    a[:, :, 0, :, 0] = 1.96875
    x[:, :, 8:] = a * np.exp2(rng.integers(-2, 3, (N, 8, 1, C, 1)))
    return x
def undecided(u):
    u = u.reshape(N, 128, 128, 4)
    u[:, :, ::16] = 0
    u[:, :, 1:4] = 0
    return u
def setup_inputs(rng):
    return {**numbers_of(rng), "ch": changes(rng), **weights(rng, layers(rng))}
def setup_inputs_ties(rng):
    d = numbers_of(rng)
    x = edges(rng, d["x"])
    k = rng.integers(-1, 2, (N, 8, C)).astype(np.float32)
    o = rng.permutation(N)
    k[o[0]] = 0
    k[o[1]] = rng.integers(0, 2, (8, 1)) * 2.0 - 1.0
    x[:, :, 0] = 0
    x[:, :, 0, :, 0] = k
    u = undecided(d["u"])
    for h in range(0, 128, 16): u[:, h, h, 0] = 1.0
    for b in range(3): u[:, 16 * b, 1 + b, 0] = 1.0
    return {"x": x.reshape(N, 128, 4 * C).astype(BF), "u": u.reshape(N, 128, 512), "v": d["v"], "ch": changes(rng), **weights(rng, layers(rng, [0]))}
def setup_inputs_near(rng):
    d = numbers_of(rng)
    x = d["x"].astype(np.float32).reshape(N, 8, 16, C, 4)
    s = rng.integers(0, 256, (N, 8, C))
    x[:, :, 0] = 0
    x[:, :, 8:] = 0
    x[:, :, 0, :, 0] = rng.integers(0, 2, (N, 8, C)) * 2.0 - 1.0
    for i in range(2): x[:, :, 8 + i] = ((s[:, :, :, None] >> (4 * i + np.arange(4))) & 1) * np.exp2(4.0 * i + np.arange(4) - 23.0)
    x[:, :, 11, :, 0] = 2.0 ** -10
    x[:, :, 12, :, :3] = rng.integers(-1, 2, (N, 8, C, 3)) * 2.0 ** -22
    o = rng.permutation(N) % 4
    x[o == 3, :, 8:] *= np.float32(2.0 ** -7)
    x[o == 3, :, 12:13] *= np.float32(0.5)
    u = undecided(d["u"])
    for r in range(N):
        k = 1.0 if o[r] == 0 else 2.0 ** -30
        for h in range(0, 128, 16):
            u[r, h + 8:h + 10, h] = k
            if o[r] < 2:
                u[r, h, h, 0] = k
                u[r, h + 11, h, 0] = k
        for b in range(3): u[r, 16 * b + 12, 1 + b, b] = k
    return {"x": x.reshape(N, 128, 4 * C).astype(BF), "u": u.reshape(N, 128, 512), "v": d["v"], "ch": changes(rng), **weights(rng, layers(rng, [0, 8, 9, 10, 11, 12, 13, 14, 15]))}
def setup_inputs_calls(rng):
    d = numbers_of(rng)
    x = edges(rng, d["x"])
    x[:, :, 0] = (-(1.0 + 0.125 * rng.permutation(N)) * 2.0 ** -6)[:, None, None, None]
    o = rng.permutation(N) % 2 * 2.0 - 1.0
    u = d["u"].reshape(N, 128, 128, 4)
    u[:, :, 1:4] = 0
    for r in range(N):
        for b in range(3): u[r, 16 * b, 1 + b, b] = float(o[r])
    return {"x": x.reshape(N, 128, 4 * C).astype(BF), "u": u.reshape(N, 128, 512), "v": d["v"], "ch": changes(rng), **weights(rng, layers(rng))}
def setup_inputs_ends(rng):
    d = numbers_of(rng)
    o = np.array([0, 2, 3, 1])[(np.arange(N) + rng.integers(4)) % 4]
    x = 2.0 ** 25 * (1.0 - 0.125 * rng.integers(0, 3, (N, 8, 16, C, 4)))
    x = np.where((o < 2)[:, None, None, None, None], x, 2.0 ** -30 * (1.0 + 0.125 * rng.integers(0, 8, (N, 1, 1, C, 1))))
    x[o == 1] *= rng.integers(0, 2, (1, 1, 1, C, 1)) * 2.0 - 1.0
    u = d["u"].astype(np.float32).reshape(N, 128, 128, 4)
    v = np.zeros((N, 128, 512), np.float32)
    w = np.zeros((N, 128, 4, 128, 4), np.float32)
    i, e = np.arange(128), np.arange(8)
    for r in range(N):
        a = 2.0 ** 30 if o[r] < 2 else 2.0 ** -30
        k = np.full((128, 8, 4), a)
        if o[r] < 2: k *= 1.0 - 0.125 * rng.integers(0, 3, (128, 8, 4))
        t = np.ones(8) if o[r] == 2 else rng.permutation(8) % 2 * 2.0 - 1.0
        u[r][:, ::16] = k * t[None, :, None]
        if o[r] > 1: u[r][:, 16 * rng.permutation(8)[:2]] = 0
        u[r][:, 1:4] = -a if o[r] == 3 else a
        v[r] = a * (rng.integers(0, 2, (128, 512)) * 2.0 - 1.0)
        if o[r] % 2 == 0: w[r] = 0.125
        else:
            for b in range(4): w[r, i, b, i, b] = 64.0 if o[r] == 1 else 2.0 ** -30
    ch = changes(rng)
    ch[o == 0] = (e + 1) % 8
    ch[o == 1] = e
    ch[o == 2] = 7 - e
    return {"x": x.astype(np.float32).reshape(N, 128, 4 * C).astype(BF), "u": u.reshape(N, 128, 512).astype(BF), "v": v.astype(BF), "ch": ch, **weights(rng, w.astype(BF))}
def setup_inputs_spread(rng):
    d = setup_inputs(rng)
    d["x"] = wide(rng, N, 128, 4 * C, cols=6)
    return d
def check_inputs(d):
    b = []
    for k, most in (("x", 2.0 ** 25), ("u", 2.0 ** 30), ("v", 2.0 ** 30)):
        a = np.abs(d[k].astype(np.float32))
        if not (np.isfinite(a).all() and ((a == 0) | (a >= 2.0 ** -30) & (a <= most)).all()): b.append("a value of " + k)
    if not (np.sort(d["ch"], axis=2) == np.arange(8)).all(): b.append("a row of ch")
    none, least, most = [emit(mx_ref.quantize(np.full((128, 16), k, np.float32).astype(BF)))[1][0, 0] for k in (0.0, 2.0 ** -30, 2.0 ** 30)]
    for r in range(N):
        if ((d["wc"][r] == 0x7F) | (d["wc"][r] == 0xFF)).any(): b.append("wc: a code that is no number")
        s = mx_ref.live(d["ws"][r])
        if ((s != none) & ((s < least) | (s > most))).any(): b.append("ws: a scale out of range")
        a = np.abs(decode(pk(d["wc"][r], d["ws"][r])).astype(np.float64)).reshape(128, 512, 4)
        if not (np.sum(a, axis=(0, 2)) <= 64).all(): b.append("sizes in a column of W")
    return b
def reference(x, u, v, ch, wc, ws):
    qu = [mx_ref.quantize(u[r]) for r in range(N)]
    lay = [pk(wc[r], ws[r]) for r in range(N)]
    now = [x[r] for r in range(N)]
    last = [None] * N
    for d in DIST:
        rung = []
        for r in range(N):
            q = mx_ref.quantize(now[r])
            s = mx_ref.matmul(qu[r], q) + np.float32(0.0)
            order = np.argsort(-s[::16], axis=1, kind="stable")
            a = ch[r][4 * (s[1] > 0) + 2 * (s[2] > 0) + (s[3] > 0)]
            row = np.array(a)
            for j in range(1, C): row[j] = row[j - 1][a[j]]
            h = np.ascontiguousarray(row.T)
            c = np.take_along_axis(order, h, axis=0)
            parts = decode(q).astype(BF).reshape(8, 16, C, 4)
            rung.append(np.ascontiguousarray(parts[h, :, c].transpose(0, 2, 1, 3)).reshape(128, 4 * C))
            last[r] = h
        sent = [mx_ref.quantize(np.ascontiguousarray(rung[r][:, :4 * H])) for r in range(N)]
        for r in range(N):
            came = sent[(r - d) % N]
            own = decode(came)
            first = tile([np.maximum(mx_ref.matmul(pick(lay[r], np.arange(128 * b, 128 * b + 128)), came), np.float32(0.0)) * np.float32(0.03125) + own[:, b::4] for b in range(4)])
            now[r] = np.concatenate([first, rung[r][:, 4 * H:]], axis=1)
    y, rw = np.zeros((N, 128, C), np.float32), np.zeros((N, 8, C), np.float32)
    oc, osc = np.zeros((N, 128, 4 * C), np.uint8), np.zeros((N, 16, C), np.uint8)
    for r in range(N):
        q = mx_ref.quantize(now[r])
        y[r] = mx_ref.matmul(mx_ref.quantize(v[r]), q)
        rw[r] = last[r]
        oc[r], osc[r] = emit(q)
    return {"y": y, "rw": rw, "oc": oc, "osc": osc}

@@ -1,0 +1,498 @@
+from concourse.mybir import dt, AluOpType as Op, AxisListType, ActivationFunctionType as AF
+
+C, H = 320, 128
+DIST = [1, 2, 4]
+TB = [0, 64, 576]
+TEND = 4672
+COD, PLN, F, BF, I4, U2 = "float8_e4m3fn_x4", "uint8", "float32", "bfloat16", "int32", "uint16"
+
+SCRATCH, PART = {}, {}
+for _d, _l in ((COD, "qw 512 qu 128 qur 128 qv 128 ce 4096 cei 512 ck 512 qx 320 qba 128 qbb 128 qm 1024"),
+               (PLN, "sw 512 su 128 sur 128 sv 128 se 4096 sei 512 sk 512 sx 320 sba 128 sbb 128 smm 1024"),
+               (BF, "xt 1280 ut 512 vt 512 tv 64 one 128 zz 4680 kk 2048 hw 2560 tab 4672 win 10240 bta 512 btb 512 m0 512 m1 512 m2 768 m3 1024 m4 1280 j0 320 j1 320 tt 1280 xn 512"),
+               (I4, "ch4 4 smi 160"),
+               (U2, "smu 128 l2 32 l3 256 offa 688 offb 1024 lt 80"),
+               (F, "smf 320 io16 512 msk 512 rst 512 cap 320 cv 320 iog 512 tm 512 ts 512 i9a 128 i9b 128"
+                   " fca 144 fcb 192 fma 144 fmb 192 fsa 144 fsb 192 sm 320 sc 320 sd 320 zm 320 zs 320 ow 320 la 144 lm 320 ls 320"
+                   " ib 192 im 192 is1 192 xa 256 xb 256 t1 32 t2 32 u1 32 u2 32 cl 256 a1 128 a2 64 rwt 320 yt 320 rl 512")):
+    _w = _l.split()
+    for _i in range(0, len(_w), 2):
+        SCRATCH[_w[_i]] = ("sbuf", [128, int(_w[_i + 1])], _d)
+for _d, _l in (("smi", "pi 8 tvi 64 tvj 64 uli 8"), ("smu", "chu 8 ul 8 pmu 16 psu 16 rku 24 lr 24 lja 16 ljb 16"),
+               ("smf", "pf 24 cst 24 kt 8 z16 16 vb 24 xt1 8 xt2 24 lf 24 lg 24 lc 24 rk 24 ivb 16 a3 24 ra 24")):
+    _w, _at = _l.split(), 0
+    for _i in range(0, len(_w), 2):
+        PART[_w[_i]] = (_d, _at)
+        _at += int(_w[_i + 1])
+for _r in range(3):
+    for _n in ("qs", "ql"):
+        SCRATCH["%s%d" % (_n, _r)] = ("sbuf", [128, H], COD)
+    for _n in ("ss", "sl"):
+        SCRATCH["%s%d" % (_n, _r)] = ("sbuf", [128, H], PLN)
+for _b in range(8):
+    SCRATCH["p%d" % _b] = ("psum", [128, 512], F)
+QSEM = {"vector": "nv", "scalar": "ns", "tensor": "nt", "g": "ng"}
+SEMAPHORES = list(QSEM.values()) + ["d%d" % _i for _i in range(40)] + ["%s%d" % (_n, _r) for _r in range(3) for _n in ("ac", "as", "lc", "lp")]
+
+
+def route(topo, src, dst):
+    if topo.may_write(src, dst):
+        return None
+    able = [c for c in topo.cores_of(src) if c != src and topo.may_write(c, dst)]
+    able.sort(key=lambda c: topo.die(c) != topo.die(src))
+    return able[0], able[1]
+
+
+def engines(topo, src, dst):
+    return topo.engines(src, dst)[:8]
+
+
+def send(g, T, topo, src, dst, v, frm, to, r):
+    rid, pid = topo.addr(dst, src)
+    e = engines(topo, src, dst)
+    a, b = T[to][:], T[frm][:]
+    if v == 0:
+        a, b = a.bitcast(dt.uint8), b.bitcast(dt.uint8)
+    g.remote_dma(a, b, T.sem[("ac%d", "as%d")[v] % r], T.sem[("lc%d", "lp%d")[v] % r], pid, rid, sum(1 << i for i in e))
+    return len(e)
+
+
+def relay_program(g, core, T, topo):
+    n = len(T.cores)
+    for r, d in enumerate(DIST):
+        for i in range(n):
+            src, dst = T.cores[i], T.cores[(i + d) % n]
+            way = route(topo, src, dst)
+            if way is None or core not in way:
+                continue
+            v = way.index(core)
+            g.wait_ge(T.sem[("ac%d", "as%d")[v] % r], len(engines(topo, src, core)))
+            land = ("ql%d", "sl%d")[v] % r
+            k = send(g, T, topo, core, dst, v, land, land, r)
+            g.wait_ge(T.sem[("lc%d", "lp%d")[v] % r], k)
+
+
+def rank_program(g, core, T, topo):
+    rank = T.rank_of(core)
+    if rank is None:
+        relay_program(g, core, T, topo)
+        return
+    n = len(T.cores)
+    eng = {"vector": g.vector, "scalar": g.scalar, "tensor": g.tensor, "g": g, "sync": g.sync}
+    count = {q: 0 for q in QSEM}
+    known = {q: {} for q in eng}
+    hist, ndma, total = {}, [0], {}
+
+    def meets(a, b):
+        if a[0] >= b[1] or b[0] >= a[1] or a[2] >= b[3] or b[2] >= a[3]:
+            return False
+        return not (a[4] == b[4] and a[4] > 1 and (a[2] - b[2]) % a[4])
+
+    def bank(name):
+        return len(name) == 2 and name[0] == "p" and name[1].isdigit()
+
+    def A(name, c0, c1, step=1, p0=0, p1=128):
+        if name in PART:
+            name, k = PART[name]
+            c0, c1 = c0 + k, c1 + k
+        return {"ap": T[name][p0:p1, c0:c1:step] if step > 1 else T[name][p0:p1, c0:c1], "reg": [(name, (0, 128, 0, 512, 1) if bank(name) else (p0, p1, c0, c1, step))], "off": []}
+
+    def W(name, c0, c1, kind):
+        return {"ap": T[name][:, c0:c1].bitcast(kind), "reg": [(name, (0, 128, c0, c1, 1))], "off": []}
+
+    def I(w, o):
+        return {"ap": w["ap"].indirect(o["ap"]), "reg": w["reg"], "off": o["reg"]}
+
+    def need(q, reads, writes, goes_on=False):
+        want = {}
+        for k, views in ((0, reads), (1, writes)):
+            for v in views:
+                for kk, name, reg in [(k, a, b) for a, b in v["reg"]] + [(0, a, b) for a, b in v["off"]]:
+                    for (oreg, ok, oq, sem, val, snap) in hist.get(name, []):
+                        if not meets(reg, oreg) or not (kk or ok or bank(name) and oq != q) or goes_on and kk and oq == q:
+                            continue
+                        if want.get(sem, (0,))[0] < val:
+                            want[sem] = (val, snap)
+        for sem in sorted(want):
+            val, snap = want[sem]
+            if known[q].get(sem, 0) >= val:
+                continue
+            eng[q].wait_ge(T.sem[sem], val)
+            for s, x in snap.items():
+                known[q][s] = max(known[q].get(s, 0), x)
+            known[q][sem] = val
+
+    def note(q, reads, writes, sem, val, snap):
+        total[sem] = max(total.get(sem, 0), val)
+        for k, views in ((0, reads), (1, writes)):
+            for v in views:
+                for kk, name, reg in [(k, a, b) for a, b in v["reg"]] + [(0, a, b) for a, b in v["off"]]:
+                    h = hist.setdefault(name, [])
+                    if kk:
+                        h[:] = [e for e in h if not (e[0][0] >= reg[0] and e[0][1] <= reg[1] and e[0][2] >= reg[2] and e[0][3] <= reg[3] and (reg[4] == 1 or reg[4] == e[0][4] and (reg[2] - e[0][2]) % reg[4] == 0))]
+                    h.append((reg, kk, q, sem, val, snap))
+
+    def emit(q, call, reads, writes, goes_on=False):
+        need(q, reads, writes, goes_on)
+        count[q] += 1
+        snap = dict(known[q])
+        call().then_inc(T.sem[QSEM[q]], 1)
+        note(q, reads, writes, QSEM[q], count[q], snap)
+
+    def dma(q, out, in_, reads, writes):
+        need(q, reads, writes)
+        sem = "d%d" % ndma[0]
+        ndma[0] += 1
+        eng[q].dma_start(out, in_).then_inc(T.sem[sem], 16)
+        note("dma", reads, writes, sem, 16, dict(known[q]))
+
+    def copy(out, in_):
+        emit("vector", lambda: g.vector.tensor_copy(out["ap"], in_["ap"]), [in_], [out])
+
+    def ts(out, in_, s1, s2, o0, *o1):
+        a = [s["ap"] if isinstance(s, dict) else s for s in (s1, s2)]
+        emit("vector", lambda: g.vector.tensor_scalar(out["ap"], in_["ap"], a[0], a[1], o0, *o1), [in_] + [s for s in (s1, s2) if isinstance(s, dict)], [out])
+
+    def tt(out, a, b, o):
+        emit("vector", lambda: g.vector.tensor_tensor(out["ap"], a["ap"], b["ap"], o), [a, b], [out])
+
+    def add_runs(s, m, c0, w):
+        sv, rs, mv = A(s, c0, c0 + w), A("rst", 0, w), A(m, c0, c0 + w)
+        emit("vector", lambda: g.vector.tensor_tensor_scan(sv["ap"], rs["ap"], mv["ap"], 0.0, Op.mult, Op.add), [rs, mv], [sv])
+
+    def wrap(s, m, in_, c0, w):
+        tt(A(m, c0, c0 + w), in_, A("msk", 0, w), Op.mult)
+        add_runs(s, m, c0, w)
+
+    def fill(v, c):
+        emit("vector", lambda: g.vector.memset(v["ap"], c), [], [v])
+
+    def quant(q, s, c0, c1, src):
+        oq, os_ = A(q, c0, c1), A(s, c0, c1)
+        emit("vector", lambda: g.vector.quantize_mx(oq["ap"], os_["ap"], src["ap"]), [src], [oq, os_])
+
+    def act(out, in_, f=AF.Copy, accum=None, scale=None):
+        k = {} if scale is None else {"scale": scale}
+        if accum:
+            k["accum_out"] = accum["ap"]
+        emit("scalar", lambda: g.scalar.activation(out["ap"], in_["ap"], f, **k), [in_], [out] + ([accum] if accum else []))
+
+    def mm(b, w, sw, w0, x, sx, x0, x1, start=True, stop=True):
+        o, v = A(b, 0, x1 - x0), [A(w, w0, w0 + 128), A(sw, w0, w0 + 128), A(x, x0, x1), A(sx, x0, x1)]
+        emit("tensor", lambda: g.tensor.matmul_mx(o["ap"], v[0]["ap"], v[1]["ap"], v[2]["ap"], v[3]["ap"], start, stop), v, [o], not start)
+
+    def iota(v, pattern, base, cm, small=True):
+        k = {"allow_small_or_imprecise_dtypes": True} if small else {}
+        emit("g", lambda: g.iota(v["ap"], pattern, base, cm, **k), [], [v])
+
+    def turn32(o, i_):
+        emit("vector", lambda: g.vector.transpose(o["ap"], i_["ap"]), [i_], [o])
+
+    def exchange(x, a, b):
+        turn32(A(a, 0, 32), A(x, 0, 32))
+        copy(A(b, 0, 16), A(a, 16, 32))
+        act(A(b, 16, 32), A(a, 0, 16))
+        turn32(A(x, 32, 64), A(b, 0, 32))
+        for q in range(4):
+            (act if q % 2 else copy)(A(x, 64, 128, 1, 32 * q, 32 * q + 32), A(x, 0, 64, 1, 32 * (q ^ 1), 32 * (q ^ 1) + 32))
+        copy(A(x, 128, 256, 1, 0, 64), A(x, 0, 128, 1, 64, 128))
+        act(A(x, 128, 256, 1, 64, 128), A(x, 0, 128, 1, 0, 64))
+
+    def merge(*lists):
+        at = []
+        for k, (items, from_) in enumerate(lists):
+            at += [(from_ + (1 - from_) * (i + 0.5) / len(items), k, i) for i in range(len(items))]
+        for _, k, i in sorted(at):
+            lists[k][0][i]()
+
+    def load(q, v, src):
+        dma(q, v["ap"], src, [], [v])
+    load("sync", A("xt", 0, 1280), T.x[:])
+    load("scalar", A("ut", 0, 512), T.u[:])
+    for i in range(8):
+        load(("sync", "scalar")[i % 2], A("ch4", 0, 4, 1, 16 * i, 16 * i + 16), T.ch[:])
+    load("sync", W("qw", 0, 512, dt.uint8), T.wc[:])
+    load("sync", A("sw", 0, 512), T.ws[:])
+    load("sync", A("vt", 0, 512), T.v[:])
+
+    def pf(i):
+        return A("pf", i, i + 1)
+
+    def pi(i):
+        return A("pi", i, i + 1)
+    iota(pi(0), [[0, 1]], 0, 1, False)
+    iota(A("io16", 0, 512), [[0, 32], [1, 16]], 0, 0)
+    iota(A("uli", 0, 8), [[16, 8]], 0, 0, False)
+    iota(A("tvi", 0, 64), [[1, 4], [4, 16]], 0, 0, False)
+    fill(A("one", 0, 128), 1.0)
+    fill(A("zz", 0, 1560), 0.0)
+
+    def pattern(z, pat, base):
+        o, i_ = A("zz", 520 * z + 3, 520 * z + 515, 4), A("one", 0, 128)
+        emit("g", lambda: g.affine_select(o["ap"], i_["ap"], pat, Op.is_equal, 0.0, base, 1), [i_], [o])
+    for h in range(3):
+        pattern(h, [[0, 8], [-1, 16]], -16 * h)
+    iota(A("iog", 0, 512), [[1, 8], [0, 64]], 0, 0)
+    iota(A("vb", 0, 8), [[0, 4], [1, 2]], 0, 0)
+    iota(A("vb", 8, 16), [[0, 2], [1, 2], [0, 2]], 0, 0)
+    iota(A("vb", 16, 24), [[1, 2], [0, 4]], 0, 0)
+    iota(A("cv", 0, C), [[1, C]], 0, 0)
+    iota(A("cst", 0, 20), [[-16, 20]], 319, 0)
+    iota(A("kt", 0, 4), [[1, 4]], 0, 0)
+
+    ts(pi(1), pi(0), 15, None, Op.bitwise_and)
+    ts(pi(2), pi(0), 4, None, Op.logical_shift_right)
+    copy(pf(8), pi(0))
+    copy(A("ul", 0, 8), A("uli", 0, 8))
+    ts(pi(3), pi(1), 1, None, Op.logical_shift_right)
+    copy(pf(0), pi(1))
+    copy(pf(1), pi(2))
+    ts(pf(2), pi(3), 8.0, None, Op.mult)
+    ts(A("msk", 0, 512), A("io16", 0, 512), pf(0), None, Op.is_equal)
+    ts(A("rst", 0, 512), A("io16", 0, 512), 0.0, None, Op.not_equal)
+    ts(A("cap", 0, C), A("io16", 0, C), pf(0), 2e29, Op.is_lt, Op.mult)
+    for i, w in ((1, 4.0), (2, 2.0), (3, 1.0)):
+        ts(pf(9 + i), pf(8), float(i), w, Op.is_equal, Op.mult)
+    ts(A("cap", 0, C), A("cap", 0, C), -1e29, None, Op.add)
+    tt(pf(13), pf(10), pf(11), Op.add)
+    ts(A("tvj", 0, 64), A("tvi", 0, 64), 7, None, Op.bitwise_and)
+    tt(pf(14), pf(13), pf(12), Op.add)
+    fill(A("kk", 0, 1536), 0.0)
+    ts(A("tv", 0, 64), A("tvj", 0, 64), 4096.0, None, Op.mult)
+    quant("qu", "su", 0, 128, A("ut", 0, 512))
+    quant("qx", "sx", 0, C, A("xt", 0, 1280))
+    copy(W("qur", 0, 128, dt.uint32), I(W("qu", 0, 128, dt.uint32), A("ul", 0, 8)))
+    copy(A("sur", 0, 128), I(A("su", 0, 128), A("ul", 0, 8)))
+    ts(A("chu", 0, 4), A("ch4", 0, 4), pf(2), None, Op.add)
+    fill(A("zz", 1560, 4680), 0.0)
+    for h in range(3, 8):
+        pattern(h, [[0, 8], [-1, 16]], -16 * h)
+    pattern(8, [[-1, 128]], 0)
+    iota(A("hw", 0, 2560), [[1, 8], [0, 320]], 0, 0)
+    copy(I(A("tab", 0, 64), A("chu", 0, 4)), A("tv", 0, 64))
+    for (lst, w, b0, b1) in (("l2", 64, 0, 64), ("l3", 512, 64, 576)):
+        wrap("ts", "tm", A("tab", b0, b1), 0, w)
+        c = w // 16
+        for k in range(8):
+            ts(A(lst, c * k, c * k + c), A("ts", 15, w, 16), 1.0 / 4096, 8.0 * k, Op.mult, Op.add)
+        if w == 64:
+            copy(A("tab", 64, 576), I(A("tab", 0, 64), A(lst, 0, 32)))
+        else:
+            act(A("tab", 576, TEND), I(A("tab", 0, 64), A(lst, 0, 256)))
+    for m in range(3):
+        for d, s in [(0, 1.0)] + [(e + 1, -1.0) for e in range(m)]:
+            ts(A("kk", 512 * d + m, 512 * d + 512, 4), A("one", 0, 128), pf(14), s * 8.0 ** (m + 1), Op.mult, Op.mult)
+    ts(A("kk", 1536, 2048), A("iog", 0, 512), pf(1), -1.0, Op.is_equal, Op.mult)
+    for v in ("bta", "btb"):
+        fill(A(v, 0, 512), 0.0)
+    fill(A("z16", 0, 16), 0.0)
+    for j in range(4):
+        quant("ck", "sk", 128 * j, 128 * j + 128, A("kk", 512 * j, 512 * j + 512))
+    WID, MC = [128, 128, 192, 256, 320], [0, 128, 256, 448, 704]
+    for j in range(4, -1, -1):
+        fill(A("m%d" % j, 256 * j, 4 * WID[j]), 0.0)
+
+    def late_constants():
+        ts(pf(3), pf(1), 320.0, None, Op.mult)
+        ts(pf(4), pf(1), 4096.0, None, Op.mult)
+        ts(pf(5), pf(1), 4096.0, 4096.0, Op.mult, Op.add)
+        ts(pf(7), pf(1), -114688.0, -114688.0, Op.mult, Op.add)
+        for b in range(3):
+            ts(pi(4 + b), pi(0), 4 + b, None, Op.logical_shift_right)
+        ts(A("cv", 0, C), A("cv", 0, C), pf(3), None, Op.add)
+        for b in range(3):
+            ts(pi(4 + b), pi(4 + b), 1, None, Op.bitwise_and)
+        ts(A("cst", 0, 20), A("cst", 0, 20), pf(0), None, Op.subtract)
+        for b in range(3):
+            copy(pf(16 + b), pi(4 + b))
+        ts(A("kt", 0, 4), A("kt", 0, 4), pf(7), None, Op.add)
+        for b in range(3):
+            ts(A("xt2", 8 * b, 8 * b + 8), A("vb", 8 * b, 8 * b + 8), pf(16 + b), 32.0 * 2 ** b, Op.not_equal, Op.mult)
+        tt(A("xt2", 0, 8), A("xt2", 0, 8), A("xt2", 8, 16), Op.add)
+        fill(A("fca", 0, 144), 0.0)
+        tt(A("xt2", 0, 8), A("xt2", 0, 8), A("xt2", 16, 24), Op.add)
+        fill(A("xa", 0, 32), 0.0)
+        fill(A("xb", 0, 32), 0.0)
+        ts(A("xt1", 0, 8), A("xt2", 0, 8), pf(0), None, Op.add)
+
+    turn = [0]
+
+    def calls(c0, c1, bt, qb, sb):
+        mm("p1", "qu", "su", 0, "qx", "sx", c0, c1)
+        w = c1 - c0
+        for m in range(3):
+            k = len(range(m, w, 3))
+            ts(A(bt, m, m + 4 * k - 3, 4), A("p1", m, w, 3), 0.0, None, Op.is_gt)
+        quant(qb, sb, 0, 128, A(bt, 0, 512))
+        for j, b in enumerate(("p2", "p3", "p4")):
+            mm(b, "ck", "sk", 128 * j, qb, sb, 0, 128)
+
+    def own(bk, c0, c1):
+        w = c1 - c0
+        wrap("sc", "sm", A(bk, 0, w), c0, w)
+        tt(A("sd", c0, c1), A(bk, 0, w), A("cap", 0, w), Op.min)
+
+    def start(i9, off):
+        act(A(i9, 0, 128), A("p2", 0, 128))
+        ts(A(off, 0, 16), A("z16", 0, 16), A(i9, 0, 1), pf(1), Op.add, Op.add)
+
+    def steps(i9, off, k):
+        def one(b):
+            return lambda: ts(A(off, 16 * b + 16, 16 * b + 32), I(A("tab", TB[2], TEND), A(off, 16 * b, 16 * b + 1)), 1.0 / 4096, A(i9, b + 1, b + 2), Op.mult, Op.add)
+        return [one(b) for b in range(k - 1)]
+
+    def places(off, k, w, fc, fm, fs, lj):
+        copy(A(fc, 2 * w, 2 * w + k), A(off, 0, 16 * k, 16))
+        tt(A(fc, 0, k), A("p3", 0, k), A(fc, 2 * w, 2 * w + k), Op.add)
+        tt(A(fc, w, w + k), A("p4", 0, k), A(fc, 2 * w, 2 * w + k), Op.add)
+        wrap(fs, fm, A(fc, 0, 3 * w), 0, 3 * w)
+        for m in range(3):
+            ts(A(lj, 4 * m, 4 * m + w // 16), A(fs, w * m + 15, w * m + w, 16), float(TB[m]), None, Op.add)
+
+    def spread(first, c0, c1):
+        def one(h, b):
+            def go():
+                e = 128 * (4 * h + b)
+                if first:
+                    quant("ce", "se", e, e + 128, A("zz", 520 * h + 3 - b, 520 * h + 515 - b))
+                bk = ("p6", "p7")[turn[0] % 2]
+                turn[0] += 1
+                mm(bk, "ce", "se", e, "qx", "sx", c0, c1)
+                act(A("win", 1280 * h + 4 * c0 + b, 1280 * h + 4 * c1, 4), A(bk, 0, c1 - c0))
+            return go
+        return [one(h, b) for h in range(8) for b in range(4)]
+
+    def ge(k, src, lo, hi, base):
+        ts(A("m%d" % (k // 4), 4 * lo + k % 4, 4 * hi, 4), A(src, lo - base, hi - base), A("sc", 16 * k + 15, 16 * k + 16), None, Op.is_ge)
+
+    def add_up(k, lo, hi, to):
+        act(A("j%d" % (k % 2), lo, hi), A("m%d" % (k // 4), 4 * lo + k % 4, 4 * hi, 4), AF.Copy, accum=A(to, k, k + 1))
+
+    def compare_b(k):
+        def go():
+            if k > 8:
+                ge(k, "p5", H, 16 * k, H)
+            ge(k, "sd", 16 * k, 16 * k + 16, 0)
+            add_up(k, H, 16 * k + 16, "lg")
+            if k % 4 == 0 and k > 8:
+                j = k // 4
+                quant("qm", "smm", MC[j] + H, MC[j] + WID[j], A("m%d" % j, 4 * H, 4 * WID[j]))
+        return go
+
+    def compare_a(k):
+        def go():
+            j, hi = k // 4, min(H, 16 * k)
+            if k:
+                ge(k, "p0", 0, hi, 0)
+            if k < 8:
+                ge(k, "sd", 16 * k, 16 * k + 16, 0)
+                hi += 16
+            add_up(k, 0, hi, "lf")
+            if k % 4 == 0:
+                w = H if j > 2 else WID[j]
+                quant("qm", "smm", MC[j], MC[j] + w, A("m%d" % j, 0, 4 * w))
+                mm("p1", "ck", "sk", 384, "qm", "smm", MC[j], MC[j] + WID[j], j == 4, j == 0)
+        return go
+
+    def part_b(r):
+        calls(H, C, "btb", "qbb", "sbb")
+        mm("p5", "qur", "sur", 0, "qx", "sx", H, C)
+        own("p5", H, C)
+        start("i9b", "offb")
+        merge(([compare_b(k) for k in range(19, 7, -1)], 0.0), (steps("i9b", "offb", 64), 0.35 if r == 0 else 0.0), (spread(r == 0, H, C), 0.0))
+        tt(A("ra", 8, 20), A("lg", 8, 20), A("cst", 8, 20), Op.add)
+        places("offb", 64, 64, "fcb", "fmb", "fsb", "ljb")
+        for m in range(3):
+            copy(A("ib", m, 192, 3), I(A("tab", 0, TEND), A("ljb", 4 * m, 4 * m + 4)))
+        wrap("is1", "im", A("ib", 0, 192), 0, 192)
+        copy(A("xb", 0, 12), A("is1", 15, 192, 16))
+        exchange("xb", "u1", "u2")
+
+    def part_a(r):
+        calls(0, H, "bta", "qba", "sba")
+        mm("p0", "qur", "sur", 0, "qx", "sx", 0, H)
+        own("p0", 0, H)
+        start("i9a", "offa")
+        merge(([compare_a(k) for k in range(19, -1, -1)], 0.0), (steps("i9a", "offa", 43), 0.0), (spread(False, 0, H), 0.0))
+        ts(A("pmu", 0, 16), I(A("tab", TB[1], TB[2]), A("offa", 16 * 42, 16 * 42 + 1)), 1.0 / 4096, None, Op.mult)
+        places("offa", 43, 48, "fca", "fma", "fsa", "lja")
+        copy(A("psu", 0, 16), I(A("xt1", 0, 8), A("pmu", 0, 1)))
+        tt(A("lc", 0, 8), A("lf", 0, 8), A("cst", 0, 8), Op.add)
+        tt(A("lc", 8, 20), A("lf", 8, 20), A("ra", 8, 20), Op.add)
+        wrap("zs", "zm", A("p1", 0, C), 0, C)
+        tt(A("rk", 0, 20), A("zs", 15, C, 16), A("lc", 0, 20), Op.add)
+        copy(A("ivb", 0, 16), I(A("xb", 0, 256), A("psu", 0, 1)))
+        copy(A("rku", 0, 20), A("rk", 0, 20))
+        copy(I(A("ow", 0, C), A("rku", 0, 20)), A("cv", 0, C))
+        for m in range(3):
+            tt(A("la", m, 144, 3), I(A("tab", 0, TEND), A("lja", 4 * m, 4 * m + 3)), A("ow", m, 144, 3), Op.add)
+        tt(A("lm", H, C), A("ow", H, C), A("msk", 0, C - H), Op.mult)
+        tt(A("lm", 0, H), A("la", 0, H), A("msk", 0, H), Op.mult)
+        add_runs("ls", "lm", 0, C)
+        copy(A("xa", 0, 8), A("ls", 15, H, 16))
+        tt(A("xa", 8, 20), A("ls", H + 15, C, 16), A("ivb", 0, 12), Op.add)
+        exchange("xa", "t1", "t2")
+        ts(A("cl", 0, 256), A("xa", 0, 256), pf(4), pf(5), Op.max, Op.min)
+        tt(A("a1", 0, 128), A("cl", 0, 128), A("cl", 128, 256), Op.add)
+        tt(A("a2", 0, 64), A("a1", 0, 64), A("a1", 64, 128), Op.add)
+        tt(A("a3", 0, 20), A("a2", 0, 20), A("a2", 32, 52), Op.add)
+        for t in (2, 0, 3, 1):
+            ts(A("lt", 20 * t, 20 * t + 20), A("a3", 0, 20), 4.0, A("kt", t, t + 1), Op.mult, Op.add)
+
+    def gather(c0, c1, mine):
+        for t in (2, 0, 3, 1):
+            (copy if t in mine else act)(A("tt", 4 * c0 + t, 4 * c1, 4), I(A("win", 0, 10240), A("lt", 20 * t + c0 // 16, 20 * t + c1 // 16)))
+
+    def store(c0, c1):
+        q = W("qx", c0, c1, dt.uint8)
+        dma("sync", T.oc[:, 4 * c0:4 * c1], q["ap"], [q], [])
+        for k in range(4):
+            s = A("sx", c0, c1, 1, 32 * k, 32 * k + 4)
+            dma("sync", T.osc[4 * k:4 * k + 4, c0:c1], s["ap"], [s], [])
+        mm("p1", "qv", "sv", 0, "qx", "sx", c0, c1)
+        y = A("yt", c0, c1)
+        act(y, A("p1", 0, c1 - c0))
+        dma("scalar", T.y[:, c0:c1], y["ap"], [y], [])
+
+    late_constants()
+    part_b(0)
+    for r, d in enumerate(DIST):
+        part_a(r)
+        gather(0, H, (0, 1))
+        mine, land = ("qs%d" % r, "ss%d" % r), ("ql%d" % r, "sl%d" % r)
+        quant(mine[0], mine[1], 0, H, A("tt", 0, 4 * H))
+        dst, src = T.cores[(rank + d) % n], T.cores[(rank - d) % n]
+        way, last = route(topo, core, dst), route(topo, src, core)
+        for v in (0, 1):
+            i_ = A(mine[v], 0, H)
+            need("g", [i_], [])
+            k = send(g, T, topo, core, way[v] if way else dst, v, mine[v], land[v], r)
+            note("net", [i_], [], ("lc%d", "lp%d")[v] % r, k, dict(known["g"]))
+        gather(H, C, (0, 1))
+        quant("qx", "sx", H, C, A("tt", 4 * H, 4 * C))
+        if r < 2:
+            part_b(r + 1)
+        else:
+            ts(A("rk", 0, 20), A("a3", 0, 20), 4.0, A("kt", 0, 1), Op.mult, Op.add)
+            ts(A("lr", 0, 20), A("rk", 0, 20), 0.25, None, Op.mult)
+            copy(A("rwt", 0, C), I(A("hw", 0, 2560), A("lr", 0, 20)))
+            i_ = A("rwt", 0, C)
+            dma("sync", T.rw[:], T["rwt"][0:128:16, 0:C], [i_], [])
+            store(H, C)
+        if r == 0:
+            for b in range(4):
+                quant("cei", "sei", 128 * b, 128 * b + 128, A("zz", 4163 - b, 4675 - b))
+            quant("qv", "sv", 0, 128, A("vt", 0, 512))
+        for v in (0, 1):
+            note("net", [], [A(land[v], 0, H)], ("ac%d", "as%d")[v] % r, len(engines(topo, last[v] if last else src, core)), {})
+        pw, pe = ("p2", "p3", "p4", "p0"), ("p6", "p7", "p1", "p6")
+        for b in range(4):
+            mm(pw[b], "qw", "sw", 128 * b, land[0], land[1], 0, H)
+            mm(pe[b], "cei", "sei", 128 * b, land[0], land[1], 0, H)
+            act(A("rl", 128 * b, 128 * b + 128), A(pw[b], 0, H), AF.Relu, scale=0.03125)
+            tt(A("xn", b, 512, 4), A("rl", 128 * b, 128 * b + 128), A(pe[b], 0, H), Op.add)
+        quant("qx", "sx", 0, H, A("xn", 0, 512))
+    store(0, H)
+    for sem in sorted(total):
+        if known["g"].get(sem, 0) < total[sem]:
+            g.wait_ge(T.sem[sem], total[sem])

@@ -11,15 +11,15 @@ for _d, _l in ((COD, "qw 512 qu 128 qur 128 qv 128 ce 4096 cei 512 ck 512 qx 320
                (PLN, "sw 512 su 128 sur 128 sv 128 se 4096 sei 512 sk 512 sx 320 sba 128 sbb 128 smm 1024"),
                (BF, "xt 1280 ut 512 vt 512 tv 64 one 128 zz 4680 kk 2048 hw 2560 tab 4672 win 10240 bta 512 btb 512 m0 512 m1 512 m2 768 m3 1024 m4 1280 j0 320 j1 320 tt 1280 xn 512"),
                (I4, "ch4 4 smi 160"),
-               (U2, "smu 128 l2 32 l3 256 offa 688 offb 1024 lt 80"),
-               (F, "smf 320 io16 512 msk 512 rst 512 cap 320 cv 320 iog 512 tm 512 ts 512 i9a 128 i9b 128"
+               (U2, "smu 240 l2 32 l3 256 offa 688 offb 1024 lt 80"),
+               (F, "smf 416 io16 512 msk 512 rst 512 cap 320 cv 320 iog 512 tm 512 ts 512 i9a 384 i9b 384"
                    " fca 144 fcb 192 fma 144 fmb 192 fsa 144 fsb 192 sm 320 sc 320 sd 320 zm 320 zs 320 ow 320 la 144 lm 320 ls 320"
-                   " ib 192 im 192 is1 192 xa 256 xb 256 t1 32 t2 32 u1 32 u2 32 cl 256 a1 128 a2 64 rwt 320 yt 320 rl 512")):
+                   " ib 192 im 192 is1 192 xa 256 xb 288 t1 32 t2 32 u1 32 u2 32 cl 256 a1 128 a2 64 rwt 320 yt 320 rl 512")):
     _w = _l.split()
     for _i in range(0, len(_w), 2):
         SCRATCH[_w[_i]] = ("sbuf", [128, int(_w[_i + 1])], _d)
-for _d, _l in (("smi", "pi 8 tvi 64 tvj 64 uli 8"), ("smu", "chu 8 ul 8 pmu 16 psu 16 rku 24 lr 24 lja 16 ljb 16"),
-               ("smf", "pf 24 cst 24 kt 8 z16 16 vb 24 xt1 8 xt2 24 lf 24 lg 24 lc 24 rk 24 ivb 16 a3 24 ra 24")):
+for _d, _l in (("smi", "pi 8 tvi 64 tvj 64 uli 8"), ("smu", "chu 8 ul 8 pmu 16 psu 64 ivu 64 rku 24 lr 24 lja 16 ljb 16"),
+               ("smf", "pf 24 cst 24 kt 8 z16 16 vb 24 xt1 8 xt2 24 lf 24 lg 24 lc 24 rk 24 ivf 16 a3 24 ra 24 ends 64")):
     _w, _at = _l.split(), 0
     for _i in range(0, len(_w), 2):
         PART[_w[_i]] = (_d, _at)
@@ -189,19 +189,23 @@ def rank_program(g, core, T, topo):
         emit("vector", lambda: g.vector.transpose(o["ap"], i_["ap"]), [i_], [o])
 
     def exchange(x, a, b):
-        turn32(A(a, 0, 32), A(x, 0, 32))
-        copy(A(b, 0, 16), A(a, 16, 32))
-        act(A(b, 16, 32), A(a, 0, 16))
-        turn32(A(x, 32, 64), A(b, 0, 32))
-        for q in range(4):
-            (act if q % 2 else copy)(A(x, 64, 128, 1, 32 * q, 32 * q + 32), A(x, 0, 64, 1, 32 * (q ^ 1), 32 * (q ^ 1) + 32))
-        copy(A(x, 128, 256, 1, 0, 64), A(x, 0, 128, 1, 64, 128))
-        act(A(x, 128, 256, 1, 64, 128), A(x, 0, 128, 1, 0, 64))
+        def quarters(c0, c1):
+            for q in range(4):
+                (act if q % 2 else copy)(A(x, 64 + c0, 64 + c1, 1, 32 * q, 32 * q + 32), A(x, c0, c1, 1, 32 * (q ^ 1), 32 * (q ^ 1) + 32))
+
+        def second():
+            copy(A(b, 0, 16), A(a, 16, 32))
+            act(A(b, 16, 32), A(a, 0, 16))
+
+        def halves():
+            copy(A(x, 128, 256, 1, 0, 64), A(x, 0, 128, 1, 64, 128))
+            act(A(x, 128, 256, 1, 64, 128), A(x, 0, 128, 1, 0, 64))
+        return [lambda: turn32(A(a, 0, 32), A(x, 0, 32)), second, lambda: turn32(A(x, 32, 64), A(b, 0, 32)), lambda: quarters(0, 64), halves]
 
     def merge(*lists):
         at = []
-        for k, (items, from_) in enumerate(lists):
-            at += [(from_ + (1 - from_) * (i + 0.5) / len(items), k, i) for i in range(len(items))]
+        for k, (items, f0, f1) in enumerate(lists):
+            at += [(f0 + (f1 - f0) * (i + 0.5) / len(items), k, i) for i in range(len(items))]
         for _, k, i in sorted(at):
             lists[k][0][i]()
 
@@ -221,133 +225,117 @@ def rank_program(g, core, T, topo):
     def pi(i):
         return A("pi", i, i + 1)
     iota(pi(0), [[0, 1]], 0, 1, False)
-    iota(A("io16", 0, 512), [[0, 32], [1, 16]], 0, 0)
     iota(A("uli", 0, 8), [[16, 8]], 0, 0, False)
     iota(A("tvi", 0, 64), [[1, 4], [4, 16]], 0, 0, False)
+    iota(A("io16", 0, 512), [[0, 32], [1, 16]], 0, 0)
     fill(A("one", 0, 128), 1.0)
     fill(A("zz", 0, 1560), 0.0)
 
     def pattern(z, pat, base):
         o, i_ = A("zz", 520 * z + 3, 520 * z + 515, 4), A("one", 0, 128)
         emit("g", lambda: g.affine_select(o["ap"], i_["ap"], pat, Op.is_equal, 0.0, base, 1), [i_], [o])
+    iota(A("iog", 0, 512), [[1, 8], [0, 64]], 0, 0)
+    iota(A("cv", 0, C), [[1, C]], 0, 0)
+    iota(A("cst", 0, 20), [[-16, 20]], 319, 0)
     for h in range(3):
         pattern(h, [[0, 8], [-1, 16]], -16 * h)
-    iota(A("iog", 0, 512), [[1, 8], [0, 64]], 0, 0)
     iota(A("vb", 0, 8), [[0, 4], [1, 2]], 0, 0)
     iota(A("vb", 8, 16), [[0, 2], [1, 2], [0, 2]], 0, 0)
     iota(A("vb", 16, 24), [[1, 2], [0, 4]], 0, 0)
-    iota(A("cv", 0, C), [[1, C]], 0, 0)
-    iota(A("cst", 0, 20), [[-16, 20]], 319, 0)
     iota(A("kt", 0, 4), [[1, 4]], 0, 0)
 
     ts(pi(1), pi(0), 15, None, Op.bitwise_and)
     ts(pi(2), pi(0), 4, None, Op.logical_shift_right)
     copy(pf(8), pi(0))
     copy(A("ul", 0, 8), A("uli", 0, 8))
+    ts(A("tvj", 0, 64), A("tvi", 0, 64), 7, None, Op.bitwise_and)
     ts(pi(3), pi(1), 1, None, Op.logical_shift_right)
     copy(pf(0), pi(1))
     copy(pf(1), pi(2))
-    ts(pf(2), pi(3), 8.0, None, Op.mult)
-    ts(A("msk", 0, 512), A("io16", 0, 512), pf(0), None, Op.is_equal)
-    ts(A("rst", 0, 512), A("io16", 0, 512), 0.0, None, Op.not_equal)
-    ts(A("cap", 0, C), A("io16", 0, C), pf(0), 2e29, Op.is_lt, Op.mult)
     for i, w in ((1, 4.0), (2, 2.0), (3, 1.0)):
         ts(pf(9 + i), pf(8), float(i), w, Op.is_equal, Op.mult)
-    ts(A("cap", 0, C), A("cap", 0, C), -1e29, None, Op.add)
+    ts(pf(2), pi(3), 8.0, None, Op.mult)
+    ts(A("tv", 0, 64), A("tvj", 0, 64), 4096.0, None, Op.mult)
+    ts(A("msk", 0, 512), A("io16", 0, 512), pf(0), None, Op.is_equal)
     tt(pf(13), pf(10), pf(11), Op.add)
-    ts(A("tvj", 0, 64), A("tvi", 0, 64), 7, None, Op.bitwise_and)
+    ts(A("rst", 0, 512), A("io16", 0, 512), 0.0, None, Op.not_equal)
     tt(pf(14), pf(13), pf(12), Op.add)
     fill(A("kk", 0, 1536), 0.0)
-    ts(A("tv", 0, 64), A("tvj", 0, 64), 4096.0, None, Op.mult)
     quant("qu", "su", 0, 128, A("ut", 0, 512))
     quant("qx", "sx", 0, C, A("xt", 0, 1280))
-    copy(W("qur", 0, 128, dt.uint32), I(W("qu", 0, 128, dt.uint32), A("ul", 0, 8)))
-    copy(A("sur", 0, 128), I(A("su", 0, 128), A("ul", 0, 8)))
-    ts(A("chu", 0, 4), A("ch4", 0, 4), pf(2), None, Op.add)
-    fill(A("zz", 1560, 4680), 0.0)
+    WID, MC = [128, 128, 192, 256, 320], [0, 128, 256, 448, 704]
+
+    tabs = [lambda: ts(A("chu", 0, 4), A("ch4", 0, 4), pf(2), None, Op.add), lambda: copy(I(A("tab", 0, 64), A("chu", 0, 4)), A("tv", 0, 64))]
+
+    def lists(lst, w, k):
+        c = w // 16
+        return lambda: ts(A(lst, c * k, c * k + c), A("ts", 15, w, 16), 1.0 / 4096, 8.0 * k, Op.mult, Op.add)
+    for (lst, w, b0) in (("l2", 64, 0), ("l3", 512, 64)):
+        tabs += [lambda w=w, b0=b0: tt(A("tm", 0, w), A("tab", b0, b0 + w), A("msk", 0, w), Op.mult), lambda w=w: add_runs("ts", "tm", 0, w)]
+        tabs += [lists(lst, w, k) for k in range(8)]
+        if w == 64:
+            tabs += [lambda: copy(A("tab", 64, 576), I(A("tab", 0, 64), A("l2", 0, 32)))]
+    tabs += [lambda: act(A("tab", 576, TEND), I(A("tab", 0, 64), A("l3", 0, 256)))]
+
+    def weights(m, d, s):
+        return lambda: ts(A("kk", 512 * d + m, 512 * d + 512, 4), A("one", 0, 128), pf(14), s * 8.0 ** (m + 1), Op.mult, Op.mult)
+    consts = [lambda: copy(W("qur", 0, 128, dt.uint32), I(W("qu", 0, 128, dt.uint32), A("ul", 0, 8))), lambda: copy(A("sur", 0, 128), I(A("su", 0, 128), A("ul", 0, 8)))]
+    consts += [weights(m, d, s) for m in range(3) for d, s in [(0, 1.0)] + [(e + 1, -1.0) for e in range(m)]]
+    consts += [lambda: ts(A("kk", 1536, 2048), A("iog", 0, 512), pf(1), -1.0, Op.is_equal, Op.mult), lambda: fill(A("btb", 0, 512), 0.0), lambda: fill(A("bta", 0, 512), 0.0)]
+    consts += [lambda j=j: quant("ck", "sk", 128 * j, 128 * j + 128, A("kk", 512 * j, 512 * j + 512)) for j in range(4)]
+    consts += [lambda: ts(A("cap", 0, C), A("io16", 0, C), pf(0), 2e29, Op.is_lt, Op.mult), lambda: fill(A("z16", 0, 16), 0.0), lambda: ts(A("cap", 0, C), A("cap", 0, C), -1e29, None, Op.add)]
+    consts += [lambda j=j: fill(A("m%d" % j, 256 * j, 4 * WID[j]), 0.0) for j in range(4, -1, -1)]
+    consts += [lambda: fill(A("zz", 1560, 4680), 0.0)]
+    merge((tabs, 0.0, 1.0), (consts, 0.0, 0.9))
     for h in range(3, 8):
         pattern(h, [[0, 8], [-1, 16]], -16 * h)
     pattern(8, [[-1, 128]], 0)
     iota(A("hw", 0, 2560), [[1, 8], [0, 320]], 0, 0)
-    copy(I(A("tab", 0, 64), A("chu", 0, 4)), A("tv", 0, 64))
-    for (lst, w, b0, b1) in (("l2", 64, 0, 64), ("l3", 512, 64, 576)):
-        wrap("ts", "tm", A("tab", b0, b1), 0, w)
-        c = w // 16
-        for k in range(8):
-            ts(A(lst, c * k, c * k + c), A("ts", 15, w, 16), 1.0 / 4096, 8.0 * k, Op.mult, Op.add)
-        if w == 64:
-            copy(A("tab", 64, 576), I(A("tab", 0, 64), A(lst, 0, 32)))
-        else:
-            act(A("tab", 576, TEND), I(A("tab", 0, 64), A(lst, 0, 256)))
-    for m in range(3):
-        for d, s in [(0, 1.0)] + [(e + 1, -1.0) for e in range(m)]:
-            ts(A("kk", 512 * d + m, 512 * d + 512, 4), A("one", 0, 128), pf(14), s * 8.0 ** (m + 1), Op.mult, Op.mult)
-    ts(A("kk", 1536, 2048), A("iog", 0, 512), pf(1), -1.0, Op.is_equal, Op.mult)
-    for v in ("bta", "btb"):
-        fill(A(v, 0, 512), 0.0)
-    fill(A("z16", 0, 16), 0.0)
-    for j in range(4):
-        quant("ck", "sk", 128 * j, 128 * j + 128, A("kk", 512 * j, 512 * j + 512))
-    WID, MC = [128, 128, 192, 256, 320], [0, 128, 256, 448, 704]
-    for j in range(4, -1, -1):
-        fill(A("m%d" % j, 256 * j, 4 * WID[j]), 0.0)
 
-    def late_constants():
-        ts(pf(3), pf(1), 320.0, None, Op.mult)
-        ts(pf(4), pf(1), 4096.0, None, Op.mult)
-        ts(pf(5), pf(1), 4096.0, 4096.0, Op.mult, Op.add)
-        ts(pf(7), pf(1), -114688.0, -114688.0, Op.mult, Op.add)
-        for b in range(3):
-            ts(pi(4 + b), pi(0), 4 + b, None, Op.logical_shift_right)
-        ts(A("cv", 0, C), A("cv", 0, C), pf(3), None, Op.add)
-        for b in range(3):
-            ts(pi(4 + b), pi(4 + b), 1, None, Op.bitwise_and)
-        ts(A("cst", 0, 20), A("cst", 0, 20), pf(0), None, Op.subtract)
-        for b in range(3):
-            copy(pf(16 + b), pi(4 + b))
-        ts(A("kt", 0, 4), A("kt", 0, 4), pf(7), None, Op.add)
-        for b in range(3):
-            ts(A("xt2", 8 * b, 8 * b + 8), A("vb", 8 * b, 8 * b + 8), pf(16 + b), 32.0 * 2 ** b, Op.not_equal, Op.mult)
-        tt(A("xt2", 0, 8), A("xt2", 0, 8), A("xt2", 8, 16), Op.add)
-        fill(A("fca", 0, 144), 0.0)
-        tt(A("xt2", 0, 8), A("xt2", 0, 8), A("xt2", 16, 24), Op.add)
-        fill(A("xa", 0, 32), 0.0)
-        fill(A("xb", 0, 32), 0.0)
-        ts(A("xt1", 0, 8), A("xt2", 0, 8), pf(0), None, Op.add)
+    late = [lambda: ts(pf(3), pf(1), 320.0, None, Op.mult), lambda: ts(pf(4), pf(1), 4096.0, None, Op.mult), lambda: ts(pf(5), pf(1), 4096.0, 4096.0, Op.mult, Op.add),
+            lambda: ts(pf(7), pf(1), -114688.0, -114688.0, Op.mult, Op.add)]
+    late += [lambda b=b: ts(pi(4 + b), pi(0), 4 + b, None, Op.logical_shift_right) for b in range(3)]
+    late += [lambda: ts(A("cv", 0, C), A("cv", 0, C), pf(3), None, Op.add), lambda: fill(A("fca", 0, 144), 0.0)]
+    late += [lambda b=b: ts(pi(4 + b), pi(4 + b), 1, None, Op.bitwise_and) for b in range(3)]
+    late += [lambda: ts(A("cst", 0, 20), A("cst", 0, 20), pf(0), None, Op.subtract), lambda: fill(A("xa", 0, 32), 0.0)]
+    late += [lambda b=b: copy(pf(16 + b), pi(4 + b)) for b in range(3)]
+    late += [lambda: ts(A("kt", 0, 4), A("kt", 0, 4), pf(7), None, Op.add)]
+    late += [lambda b=b: ts(A("xt2", 8 * b, 8 * b + 8), A("vb", 8 * b, 8 * b + 8), pf(16 + b), 32.0 * 2 ** b, Op.not_equal, Op.mult) for b in range(3)]
+    late += [lambda: fill(A("xb", 0, 288), 0.0), lambda: tt(A("xt2", 0, 8), A("xt2", 0, 8), A("xt2", 8, 16), Op.add), lambda: tt(A("xt2", 0, 8), A("xt2", 0, 8), A("xt2", 16, 24), Op.add),
+             lambda: ts(A("xt1", 0, 8), A("xt2", 0, 8), pf(0), None, Op.add)]
 
     turn = [0]
 
-    def calls(c0, c1, bt, qb, sb):
+    def begin(c0, c1, bt, qb, sb, i9, off, bk, starts):
         mm("p1", "qu", "su", 0, "qx", "sx", c0, c1)
+        mm(bk, "qur", "sur", 0, "qx", "sx", c0, c1)
         w = c1 - c0
         for m in range(3):
             k = len(range(m, w, 3))
             ts(A(bt, m, m + 4 * k - 3, 4), A("p1", m, w, 3), 0.0, None, Op.is_gt)
+        tt(A("sm", c0, c1), A(bk, 0, w), A("msk", 0, w), Op.mult)
         quant(qb, sb, 0, 128, A(bt, 0, 512))
         for j, b in enumerate(("p2", "p3", "p4")):
             mm(b, "ck", "sk", 128 * j, qb, sb, 0, 128)
-
-    def own(bk, c0, c1):
-        w = c1 - c0
-        wrap("sc", "sm", A(bk, 0, w), c0, w)
+            act(A(i9, 128 * j, 128 * j + 128), A(b, 0, 128))
+        add_runs("sc", "sm", c0, w)
         tt(A("sd", c0, c1), A(bk, 0, w), A("cap", 0, w), Op.min)
+        for b in starts:
+            ts(A(off, 16 * b, 16 * b + 16), A("z16", 0, 16), A(i9, b, b + 1), pf(1), Op.add, Op.add)
 
-    def start(i9, off):
-        act(A(i9, 0, 128), A("p2", 0, 128))
-        ts(A(off, 0, 16), A("z16", 0, 16), A(i9, 0, 1), pf(1), Op.add, Op.add)
+    def step(i9, off, b):
+        return lambda: ts(A(off, 16 * b + 16, 16 * b + 32), I(A("tab", TB[2], TEND), A(off, 16 * b, 16 * b + 1)), 1.0 / 4096, A(i9, b + 1, b + 2), Op.mult, Op.add)
 
-    def steps(i9, off, k):
-        def one(b):
-            return lambda: ts(A(off, 16 * b + 16, 16 * b + 32), I(A("tab", TB[2], TEND), A(off, 16 * b, 16 * b + 1)), 1.0 / 4096, A(i9, b + 1, b + 2), Op.mult, Op.add)
-        return [one(b) for b in range(k - 1)]
+    def end(s):
+        b = 16 * s + 15
+        return lambda: ts(A("ends", 16 * s, 16 * s + 16), I(A("tab", TB[2], TEND), A("offb", 16 * b, 16 * b + 1)), 1.0 / 4096, None, Op.mult)
 
-    def places(off, k, w, fc, fm, fs, lj):
-        copy(A(fc, 2 * w, 2 * w + k), A(off, 0, 16 * k, 16))
-        tt(A(fc, 0, k), A("p3", 0, k), A(fc, 2 * w, 2 * w + k), Op.add)
-        tt(A(fc, w, w + k), A("p4", 0, k), A(fc, 2 * w, 2 * w + k), Op.add)
-        wrap(fs, fm, A(fc, 0, 3 * w), 0, 3 * w)
-        for m in range(3):
-            ts(A(lj, 4 * m, 4 * m + w // 16), A(fs, w * m + 15, w * m + w, 16), float(TB[m]), None, Op.add)
+    def places(off, i9, k, w, fc, fm, fs, lj):
+        a = [lambda: copy(A(fc, 2 * w, 2 * w + k), A(off, 0, 16 * k, 16))]
+        a += [lambda d=d: tt(A(fc, w * d, w * d + k), A(i9, 128 * d + 128, 128 * d + 128 + k), A(fc, 2 * w, 2 * w + k), Op.add) for d in (0, 1)]
+        a += [lambda: tt(A(fm, 0, 3 * w), A(fc, 0, 3 * w), A("msk", 0, 3 * w), Op.mult), lambda: add_runs(fs, fm, 0, 3 * w)]
+        a += [lambda m=m: ts(A(lj, 4 * m, 4 * m + w // 16), A(fs, w * m + 15, w * m + w, 16), float(TB[m]), None, Op.add) for m in range(3)]
+        return a
 
     def spread(first, c0, c1):
         def one(h, b):
@@ -394,44 +382,40 @@ def rank_program(g, core, T, topo):
                 mm("p1", "ck", "sk", 384, "qm", "smm", MC[j], MC[j] + WID[j], j == 4, j == 0)
         return go
 
-    def part_b(r):
-        calls(H, C, "btb", "qbb", "sbb")
-        mm("p5", "qur", "sur", 0, "qx", "sx", H, C)
-        own("p5", H, C)
-        start("i9b", "offb")
-        merge(([compare_b(k) for k in range(19, 7, -1)], 0.0), (steps("i9b", "offb", 64), 0.35 if r == 0 else 0.0), (spread(r == 0, H, C), 0.0))
-        tt(A("ra", 8, 20), A("lg", 8, 20), A("cst", 8, 20), Op.add)
-        places("offb", 64, 64, "fcb", "fmb", "fsb", "ljb")
-        for m in range(3):
-            copy(A("ib", m, 192, 3), I(A("tab", 0, TEND), A("ljb", 4 * m, 4 * m + 4)))
-        wrap("is1", "im", A("ib", 0, 192), 0, 192)
-        copy(A("xb", 0, 12), A("is1", 15, 192, 16))
-        exchange("xb", "u1", "u2")
+    def begin_b():
+        begin(H, C, "btb", "qbb", "sbb", "i9b", "offb", "p5", (0, 16, 32, 48))
 
-    def part_a(r):
-        calls(0, H, "bta", "qba", "sba")
-        mm("p0", "qur", "sur", 0, "qx", "sx", 0, H)
-        own("p0", 0, H)
-        start("i9a", "offa")
-        merge(([compare_a(k) for k in range(19, -1, -1)], 0.0), (steps("i9a", "offa", 43), 0.0), (spread(False, 0, H), 0.0))
-        ts(A("pmu", 0, 16), I(A("tab", TB[1], TB[2]), A("offa", 16 * 42, 16 * 42 + 1)), 1.0 / 4096, None, Op.mult)
-        places("offa", 43, 48, "fca", "fma", "fsa", "lja")
-        copy(A("psu", 0, 16), I(A("xt1", 0, 8), A("pmu", 0, 1)))
-        tt(A("lc", 0, 8), A("lf", 0, 8), A("cst", 0, 8), Op.add)
-        tt(A("lc", 8, 20), A("lf", 8, 20), A("ra", 8, 20), Op.add)
-        wrap("zs", "zm", A("p1", 0, C), 0, C)
-        tt(A("rk", 0, 20), A("zs", 15, C, 16), A("lc", 0, 20), Op.add)
-        copy(A("ivb", 0, 16), I(A("xb", 0, 256), A("psu", 0, 1)))
-        copy(A("rku", 0, 20), A("rk", 0, 20))
-        copy(I(A("ow", 0, C), A("rku", 0, 20)), A("cv", 0, C))
-        for m in range(3):
-            tt(A("la", m, 144, 3), I(A("tab", 0, TEND), A("lja", 4 * m, 4 * m + 3)), A("ow", m, 144, 3), Op.add)
-        tt(A("lm", H, C), A("ow", H, C), A("msk", 0, C - H), Op.mult)
-        tt(A("lm", 0, H), A("la", 0, H), A("msk", 0, H), Op.mult)
-        add_runs("ls", "lm", 0, C)
-        copy(A("xa", 0, 8), A("ls", 15, H, 16))
-        tt(A("xa", 8, 20), A("ls", H + 15, C, 16), A("ivb", 0, 12), Op.add)
-        exchange("xa", "t1", "t2")
+    def begin_a():
+        begin(0, H, "bta", "qba", "sba", "i9a", "offa", "p0", (0,))
+    cmp_b, cmp_a = [compare_b(k) for k in range(19, 7, -1)], [compare_a(k) for k in range(19, -1, -1)]
+    chain_b = [step("i9b", "offb", 16 * s + b) for b in range(15) for s in range(4)] + [end(s) for s in range(4)]
+    tail_b = places("offb", "i9b", 64, 64, "fcb", "fmb", "fsb", "ljb")
+    tail_b += [lambda m=m: copy(A("ib", m, 192, 3), I(A("tab", 0, TEND), A("ljb", 4 * m, 4 * m + 4))) for m in range(3)]
+    tail_b += [lambda: tt(A("im", 0, 192), A("ib", 0, 192), A("msk", 0, 192), Op.mult), lambda: act(A("xb", 4, 29, 8), A("ends", 0, 64, 16)), lambda: add_runs("is1", "im", 0, 192)]
+    tail_b += [lambda s=s: (act if s % 2 else copy)(A("xb", 8 * s, 8 * s + 3), A("is1", 48 * s + 15, 48 * s + 48, 16)) for s in range(4)]
+    tail_b += exchange("xb", "u1", "u2")
+    chain_a = [step("i9a", "offa", b) for b in range(42)]
+    mid = lambda: ts(A("pmu", 0, 16), I(A("tab", TB[1], TB[2]), A("offa", 16 * 42, 16 * 42 + 1)), 1.0 / 4096, None, Op.mult)
+    tail_a = places("offa", "i9a", 43, 48, "fca", "fma", "fsa", "lja")
+    way_b = []
+    for s in range(4):
+        at = A("ivu", 16 * s - 12, 16 * s - 11) if s else A("pmu", 0, 1)
+        way_b += [lambda s=s, at=at: copy(A("psu", 16 * s, 16 * s + 16), I(A("xt1", 0, 8), at)),
+                  lambda s=s: copy(A("ivu", 16 * s, 16 * s + 16), I(A("xb", 8 * s, 8 * s + 248), A("psu", 16 * s, 16 * s + 1)))]
+    rank_ = [lambda: tt(A("zm", 0, C), A("p1", 0, C), A("msk", 0, C), Op.mult), lambda: tt(A("lc", 8, 20), A("lf", 8, 20), A("lg", 8, 20), Op.add), lambda: add_runs("zs", "zm", 0, C),
+             lambda: copy(A("lc", 0, 8), A("lf", 0, 8)), lambda: tt(A("ra", 0, 20), A("lc", 0, 20), A("cst", 0, 20), Op.add),
+             lambda: tt(A("rk", 0, 20), A("zs", 15, C, 16), A("ra", 0, 20), Op.add), lambda: copy(A("rku", 0, 20), A("rk", 0, 20)), lambda: copy(I(A("ow", 0, C), A("rku", 0, 20)), A("cv", 0, C)),
+             lambda: tt(A("lm", H, C), A("ow", H, C), A("msk", 0, C - H), Op.mult)]
+
+    def finish():
+        parts = [lambda m=m: tt(A("la", m, 144, 3), I(A("tab", 0, TEND), A("lja", 4 * m, 4 * m + 3)), A("ow", m, 144, 3), Op.add) for m in range(3)]
+        parts += [lambda: tt(A("lm", 0, H), A("la", 0, H), A("msk", 0, H), Op.mult), lambda: add_runs("ls", "lm", 0, C), lambda: act(A("xa", 0, 8), A("ls", 15, H, 16))]
+        merge((parts, 0.0, 1.0), (way_b, 0.0, 1.0))
+        for s in range(4):
+            (act if s % 2 else copy)(A("ivf", 3 * s, 3 * s + 3), A("ivu", 16 * s, 16 * s + 3)) if s % 2 == 0 else copy(A("ivf", 3 * s, 3 * s + 3), A("ivu", 16 * s, 16 * s + 3))
+        tt(A("xa", 8, 20), A("ls", H + 15, C, 16), A("ivf", 0, 12), Op.add)
+        for f in exchange("xa", "t1", "t2"):
+            f()
         ts(A("cl", 0, 256), A("xa", 0, 256), pf(4), pf(5), Op.max, Op.min)
         tt(A("a1", 0, 128), A("cl", 0, 128), A("cl", 128, 256), Op.add)
         tt(A("a2", 0, 64), A("a1", 0, 64), A("a1", 64, 128), Op.add)
@@ -454,10 +438,14 @@ def rank_program(g, core, T, topo):
         act(y, A("p1", 0, c1 - c0))
         dma("scalar", T.y[:, c0:c1], y["ap"], [y], [])
 
-    late_constants()
-    part_b(0)
+    begin_b()
+    begin_a()
+    merge((cmp_b + cmp_a + rank_, 0.0, 1.0), (late, 0.0, 0.5), (chain_b, 0.25, 0.8), (chain_a, 0.25, 0.85), (spread(True, 0, C), 0.0, 0.95), (tail_b, 0.8, 1.0), ([mid] + tail_a, 0.85, 1.0))
     for r, d in enumerate(DIST):
-        part_a(r)
+        if r:
+            begin_a()
+            merge((cmp_a, 0.0, 0.75), (rank_, 0.75, 1.0), (chain_a, 0.0, 0.85), (spread(False, 0, H), 0.0, 0.9), (tail_b, 0.1, 0.8), ([mid] + tail_a, 0.85, 1.0))
+        finish()
         gather(0, H, (0, 1))
         mine, land = ("qs%d" % r, "ss%d" % r), ("ql%d" % r, "sl%d" % r)
         quant(mine[0], mine[1], 0, H, A("tt", 0, 4 * H))
@@ -471,7 +459,8 @@ def rank_program(g, core, T, topo):
         gather(H, C, (0, 1))
         quant("qx", "sx", H, C, A("tt", 4 * H, 4 * C))
         if r < 2:
-            part_b(r + 1)
+            begin_b()
+            merge((cmp_b, 0.0, 1.0), (chain_b, 0.0, 1.0), (spread(False, H, C), 0.0, 1.0))
         else:
             ts(A("rk", 0, 20), A("a3", 0, 20), 4.0, A("kt", 0, 1), Op.mult, Op.add)
             ts(A("lr", 0, 20), A("rk", 0, 20), 0.25, None, Op.mult)

@@ -160,10 +160,6 @@ def rank_program(g, core, T, topo):
         sv, rs, mv = A(s, c0, c0 + w), A("rst", 0, w), A(m, c0, c0 + w)
         emit("vector", lambda: g.vector.tensor_tensor_scan(sv["ap"], rs["ap"], mv["ap"], 0.0, Op.mult, Op.add), [rs, mv], [sv])
 
-    def wrap(s, m, in_, c0, w):
-        tt(A(m, c0, c0 + w), in_, A("msk", 0, w), Op.mult)
-        add_runs(s, m, c0, w)
-
     def fill(v, c):
         emit("vector", lambda: g.vector.memset(v["ap"], c), [], [v])
 
@@ -189,9 +185,9 @@ def rank_program(g, core, T, topo):
         emit("vector", lambda: g.vector.transpose(o["ap"], i_["ap"]), [i_], [o])
 
     def exchange(x, a, b):
-        def quarters(c0, c1):
+        def quarters():
             for q in range(4):
-                (act if q % 2 else copy)(A(x, 64 + c0, 64 + c1, 1, 32 * q, 32 * q + 32), A(x, c0, c1, 1, 32 * (q ^ 1), 32 * (q ^ 1) + 32))
+                (act if q % 2 else copy)(A(x, 64, 128, 1, 32 * q, 32 * q + 32), A(x, 0, 64, 1, 32 * (q ^ 1), 32 * (q ^ 1) + 32))
 
         def second():
             copy(A(b, 0, 16), A(a, 16, 32))
@@ -200,14 +196,32 @@ def rank_program(g, core, T, topo):
         def halves():
             copy(A(x, 128, 256, 1, 0, 64), A(x, 0, 128, 1, 64, 128))
             act(A(x, 128, 256, 1, 64, 128), A(x, 0, 128, 1, 0, 64))
-        return [lambda: turn32(A(a, 0, 32), A(x, 0, 32)), second, lambda: turn32(A(x, 32, 64), A(b, 0, 32)), lambda: quarters(0, 64), halves]
+        return [lambda: turn32(A(a, 0, 32), A(x, 0, 32)), second, lambda: turn32(A(x, 32, 64), A(b, 0, 32)), quarters, halves]
 
-    def merge(*lists):
-        at = []
-        for k, (items, f0, f1) in enumerate(lists):
-            at += [(f0 + (f1 - f0) * (i + 0.5) / len(items), k, i) for i in range(len(items))]
-        for _, k, i in sorted(at):
-            lists[k][0][i]()
+    LAG, CMP = 0.1, 0.25
+
+    def merge(side, gap, *strands):
+        todo = [[(f, c, w) for items, c, w in s for f in items] for s in strands]
+        left = [sum(c + w for _, c, w in s) for s in todo]
+        free, now, due = [0.0] * len(todo), 0.0, 0.0
+        side = list(side)
+        while any(todo):
+            while side and due <= now:
+                side.pop(0)()
+                due += gap
+            live = [k for k in range(len(todo)) if todo[k]]
+            able = [k for k in live if free[k] <= now]
+            if not able:
+                now = min(free[k] for k in live)
+                continue
+            k = max(able, key=lambda j: left[j])
+            f, c, w = todo[k].pop(0)
+            f()
+            now += c
+            free[k] = now + w
+            left[k] -= c + w
+        for f in side:
+            f()
 
     def load(q, v, src):
         dma(q, v["ap"], src, [], [v])
@@ -229,7 +243,7 @@ def rank_program(g, core, T, topo):
     iota(A("tvi", 0, 64), [[1, 4], [4, 16]], 0, 0, False)
     iota(A("io16", 0, 512), [[0, 32], [1, 16]], 0, 0)
     fill(A("one", 0, 128), 1.0)
-    fill(A("zz", 0, 1560), 0.0)
+    fill(A("zz", 0, 4680), 0.0)
 
     def pattern(z, pat, base):
         o, i_ = A("zz", 520 * z + 3, 520 * z + 515, 4), A("one", 0, 128)
@@ -237,12 +251,14 @@ def rank_program(g, core, T, topo):
     iota(A("iog", 0, 512), [[1, 8], [0, 64]], 0, 0)
     iota(A("cv", 0, C), [[1, C]], 0, 0)
     iota(A("cst", 0, 20), [[-16, 20]], 319, 0)
-    for h in range(3):
+    for h in range(8):
         pattern(h, [[0, 8], [-1, 16]], -16 * h)
+    pattern(8, [[-1, 128]], 0)
     iota(A("vb", 0, 8), [[0, 4], [1, 2]], 0, 0)
     iota(A("vb", 8, 16), [[0, 2], [1, 2], [0, 2]], 0, 0)
     iota(A("vb", 16, 24), [[1, 2], [0, 4]], 0, 0)
     iota(A("kt", 0, 4), [[1, 4]], 0, 0)
+    iota(A("hw", 0, 2560), [[1, 8], [0, 320]], 0, 0)
 
     ts(pi(1), pi(0), 15, None, Op.bitwise_and)
     ts(pi(2), pi(0), 4, None, Op.logical_shift_right)
@@ -277,20 +293,21 @@ def rank_program(g, core, T, topo):
             tabs += [lambda: copy(A("tab", 64, 576), I(A("tab", 0, 64), A("l2", 0, 32)))]
     tabs += [lambda: act(A("tab", 576, TEND), I(A("tab", 0, 64), A("l3", 0, 256)))]
 
-    def weights(m, d, s):
-        return lambda: ts(A("kk", 512 * d + m, 512 * d + 512, 4), A("one", 0, 128), pf(14), s * 8.0 ** (m + 1), Op.mult, Op.mult)
-    consts = [lambda: copy(W("qur", 0, 128, dt.uint32), I(W("qu", 0, 128, dt.uint32), A("ul", 0, 8))), lambda: copy(A("sur", 0, 128), I(A("su", 0, 128), A("ul", 0, 8)))]
-    consts += [weights(m, d, s) for m in range(3) for d, s in [(0, 1.0)] + [(e + 1, -1.0) for e in range(m)]]
-    consts += [lambda: ts(A("kk", 1536, 2048), A("iog", 0, 512), pf(1), -1.0, Op.is_equal, Op.mult), lambda: fill(A("btb", 0, 512), 0.0), lambda: fill(A("bta", 0, 512), 0.0)]
-    consts += [lambda j=j: quant("ck", "sk", 128 * j, 128 * j + 128, A("kk", 512 * j, 512 * j + 512)) for j in range(4)]
-    consts += [lambda: ts(A("cap", 0, C), A("io16", 0, C), pf(0), 2e29, Op.is_lt, Op.mult), lambda: fill(A("z16", 0, 16), 0.0), lambda: ts(A("cap", 0, C), A("cap", 0, C), -1e29, None, Op.add)]
-    consts += [lambda j=j: fill(A("m%d" % j, 256 * j, 4 * WID[j]), 0.0) for j in range(4, -1, -1)]
-    consts += [lambda: fill(A("zz", 1560, 4680), 0.0)]
-    merge((tabs, 0.0, 1.0), (consts, 0.0, 0.9))
-    for h in range(3, 8):
-        pattern(h, [[0, 8], [-1, 16]], -16 * h)
-    pattern(8, [[-1, 128]], 0)
-    iota(A("hw", 0, 2560), [[1, 8], [0, 320]], 0, 0)
+    copy(W("qur", 0, 128, dt.uint32), I(W("qu", 0, 128, dt.uint32), A("ul", 0, 8)))
+    copy(A("sur", 0, 128), I(A("su", 0, 128), A("ul", 0, 8)))
+    for m in range(3):
+        for d, s in [(0, 1.0)] + [(e + 1, -1.0) for e in range(m)]:
+            ts(A("kk", 512 * d + m, 512 * d + 512, 4), A("one", 0, 128), pf(14), s * 8.0 ** (m + 1), Op.mult, Op.mult)
+    ts(A("kk", 1536, 2048), A("iog", 0, 512), pf(1), -1.0, Op.is_equal, Op.mult)
+    fill(A("btb", 0, 512), 0.0)
+    fill(A("bta", 0, 512), 0.0)
+    for j in range(4):
+        quant("ck", "sk", 128 * j, 128 * j + 128, A("kk", 512 * j, 512 * j + 512))
+    ts(A("cap", 0, C), A("io16", 0, C), pf(0), 2e29, Op.is_lt, Op.mult)
+    fill(A("z16", 0, 16), 0.0)
+    ts(A("cap", 0, C), A("cap", 0, C), -1e29, None, Op.add)
+    for j in range(4, -1, -1):
+        fill(A("m%d" % j, 256 * j, 4 * WID[j]), 0.0)
 
     late = [lambda: ts(pf(3), pf(1), 320.0, None, Op.mult), lambda: ts(pf(4), pf(1), 4096.0, None, Op.mult), lambda: ts(pf(5), pf(1), 4096.0, 4096.0, Op.mult, Op.add),
             lambda: ts(pf(7), pf(1), -114688.0, -114688.0, Op.mult, Op.add)]
@@ -337,13 +354,13 @@ def rank_program(g, core, T, topo):
         a += [lambda m=m: ts(A(lj, 4 * m, 4 * m + w // 16), A(fs, w * m + 15, w * m + w, 16), float(TB[m]), None, Op.add) for m in range(3)]
         return a
 
-    def spread(first, c0, c1):
+    def spread(first, c0, c1, banks):
         def one(h, b):
             def go():
                 e = 128 * (4 * h + b)
                 if first:
                     quant("ce", "se", e, e + 128, A("zz", 520 * h + 3 - b, 520 * h + 515 - b))
-                bk = ("p6", "p7")[turn[0] % 2]
+                bk = banks[turn[0] % len(banks)]
                 turn[0] += 1
                 mm(bk, "ce", "se", e, "qx", "sx", c0, c1)
                 act(A("win", 1280 * h + 4 * c0 + b, 1280 * h + 4 * c1, 4), A(bk, 0, c1 - c0))
@@ -395,8 +412,8 @@ def rank_program(g, core, T, topo):
     tail_b += [lambda s=s: (act if s % 2 else copy)(A("xb", 8 * s, 8 * s + 3), A("is1", 48 * s + 15, 48 * s + 48, 16)) for s in range(4)]
     tail_b += exchange("xb", "u1", "u2")
     chain_a = [step("i9a", "offa", b) for b in range(42)]
-    mid = lambda: ts(A("pmu", 0, 16), I(A("tab", TB[1], TB[2]), A("offa", 16 * 42, 16 * 42 + 1)), 1.0 / 4096, None, Op.mult)
-    tail_a = places("offa", "i9a", 43, 48, "fca", "fma", "fsa", "lja")
+    chain_a += [lambda: ts(A("pmu", 0, 16), I(A("tab", TB[1], TB[2]), A("offa", 16 * 42, 16 * 42 + 1)), 1.0 / 4096, None, Op.mult)]
+    chain_a += places("offa", "i9a", 43, 48, "fca", "fma", "fsa", "lja")
     way_b = []
     for s in range(4):
         at = A("ivu", 16 * s - 12, 16 * s - 11) if s else A("pmu", 0, 1)
@@ -410,9 +427,9 @@ def rank_program(g, core, T, topo):
     def finish():
         parts = [lambda m=m: tt(A("la", m, 144, 3), I(A("tab", 0, TEND), A("lja", 4 * m, 4 * m + 3)), A("ow", m, 144, 3), Op.add) for m in range(3)]
         parts += [lambda: tt(A("lm", 0, H), A("la", 0, H), A("msk", 0, H), Op.mult), lambda: add_runs("ls", "lm", 0, C), lambda: act(A("xa", 0, 8), A("ls", 15, H, 16))]
-        merge((parts, 0.0, 1.0), (way_b, 0.0, 1.0))
+        merge([], 1.0, [(parts, 0.25, LAG)], [(way_b, 0.07, LAG)])
         for s in range(4):
-            (act if s % 2 else copy)(A("ivf", 3 * s, 3 * s + 3), A("ivu", 16 * s, 16 * s + 3)) if s % 2 == 0 else copy(A("ivf", 3 * s, 3 * s + 3), A("ivu", 16 * s, 16 * s + 3))
+            copy(A("ivf", 3 * s, 3 * s + 3), A("ivu", 16 * s, 16 * s + 3))
         tt(A("xa", 8, 20), A("ls", H + 15, C, 16), A("ivf", 0, 12), Op.add)
         for f in exchange("xa", "t1", "t2"):
             f()
@@ -423,9 +440,9 @@ def rank_program(g, core, T, topo):
         for t in (2, 0, 3, 1):
             ts(A("lt", 20 * t, 20 * t + 20), A("a3", 0, 20), 4.0, A("kt", t, t + 1), Op.mult, Op.add)
 
-    def gather(c0, c1, mine):
+    def gather(c0, c1):
         for t in (2, 0, 3, 1):
-            (copy if t in mine else act)(A("tt", 4 * c0 + t, 4 * c1, 4), I(A("win", 0, 10240), A("lt", 20 * t + c0 // 16, 20 * t + c1 // 16)))
+            (copy if t < 2 else act)(A("tt", 4 * c0 + t, 4 * c1, 4), I(A("win", 0, 10240), A("lt", 20 * t + c0 // 16, 20 * t + c1 // 16)))
 
     def store(c0, c1):
         q = W("qx", c0, c1, dt.uint8)
@@ -440,13 +457,17 @@ def rank_program(g, core, T, topo):
 
     begin_b()
     begin_a()
-    merge((cmp_b + cmp_a + rank_, 0.0, 1.0), (late, 0.0, 0.5), (chain_b, 0.25, 0.8), (chain_a, 0.25, 0.85), (spread(True, 0, C), 0.0, 0.95), (tail_b, 0.8, 1.0), ([mid] + tail_a, 0.85, 1.0))
+    wide = spread(True, 0, C, ("p6", "p7", "p2", "p3", "p4"))
+    pause = ([lambda: None], 0.0, 5.0)
+    merge(wide[:10], 0.7, [(tabs, 0.07, LAG)], [(late, 0.06, 0.0)], [(cmp_b, CMP, 0.0)])
+    merge(wide[10:], 0.4, [(cmp_a, CMP, 0.0), (rank_, 0.3, LAG)], [pause, (chain_a, 0.07, LAG)], [pause, (chain_b, 0.07, 0.0), (tail_b, 0.1, LAG)])
+    rest_b, wide = [], []
     for r, d in enumerate(DIST):
         if r:
             begin_a()
-            merge((cmp_a, 0.0, 0.75), (rank_, 0.75, 1.0), (chain_a, 0.0, 0.85), (spread(False, 0, H), 0.0, 0.9), (tail_b, 0.1, 0.8), ([mid] + tail_a, 0.85, 1.0))
+            merge(wide + spread(False, 0, H, ("p6", "p7", "p2", "p3", "p4")), 0.2, [(rest_b, CMP, 0.0), (cmp_a, CMP, 0.0), (rank_, 0.3, LAG)], [(chain_a, 0.07, LAG)], [(tail_b, 0.1, LAG)])
         finish()
-        gather(0, H, (0, 1))
+        gather(0, H)
         mine, land = ("qs%d" % r, "ss%d" % r), ("ql%d" % r, "sl%d" % r)
         quant(mine[0], mine[1], 0, H, A("tt", 0, 4 * H))
         dst, src = T.cores[(rank + d) % n], T.cores[(rank - d) % n]
@@ -456,11 +477,13 @@ def rank_program(g, core, T, topo):
             need("g", [i_], [])
             k = send(g, T, topo, core, way[v] if way else dst, v, mine[v], land[v], r)
             note("net", [i_], [], ("lc%d", "lp%d")[v] % r, k, dict(known["g"]))
-        gather(H, C, (0, 1))
+        gather(H, C)
         quant("qx", "sx", H, C, A("tt", 4 * H, 4 * C))
         if r < 2:
             begin_b()
-            merge((cmp_b, 0.0, 1.0), (chain_b, 0.0, 1.0), (spread(False, H, C), 0.0, 1.0))
+            wide = spread(False, H, C, ("p6", "p7", "p2", "p3", "p4"))
+            merge(wide[:28], 0.2, [(cmp_b[:9], CMP, 0.0)], [(chain_b, 0.07, 0.02)])
+            rest_b, wide = cmp_b[9:], wide[28:]
         else:
             ts(A("rk", 0, 20), A("a3", 0, 20), 4.0, A("kt", 0, 1), Op.mult, Op.add)
             ts(A("lr", 0, 20), A("rk", 0, 20), 0.25, None, Op.mult)

from concourse.mybir import dt, AluOpType as Op, AxisListType, ActivationFunctionType as AF

C, H = 320, 128
DIST = [1, 2, 4]
TB = [0, 64, 576]
TEND = 4672
COD, PLN, F, BF, I4, U2 = "float8_e4m3fn_x4", "uint8", "float32", "bfloat16", "int32", "uint16"

SCRATCH, PART = {}, {}
for _d, _l in ((COD, "qw 512 qu 128 qur 128 qv 128 ce 4096 cei 512 ck 512 qx 320 qba 128 qbb 128 qm 1024"),
               (PLN, "sw 512 su 128 sur 128 sv 128 se 4096 sei 512 sk 512 sx 320 sba 128 sbb 128 smm 1024"),
               (BF, "xt 1280 ut 512 vt 512 tv 64 one 128 zz 4680 kk 2048 hw 2560 tab 4672 win 10240 bta 512 btb 512 m0 512 m1 512 m2 768 m3 1024 m4 1280 j0 320 j1 320 tt 1280 xn 512"),
               (I4, "ch4 4 smi 160"),
               (U2, "smu 240 l2 32 l3 256 offa 688 offb 1024 lt 80"),
               (F, "smf 416 io16 512 msk 512 rst 512 cap 320 cv 320 iog 512 tm 512 ts 512 i9a 384 i9b 384"
                   " fca 144 fcb 192 fma 144 fmb 192 fsa 144 fsb 192 sm 320 sc 320 sd 320 zm 320 zs 320 ow 320 la 144 lm 320 ls 320"
                   " ib 192 im 192 is1 192 xa 256 xb 288 t1 32 t2 32 u1 32 u2 32 cl 256 a1 128 a2 64 rwt 320 yt 320 rl 512")):
    _w = _l.split()
    for _i in range(0, len(_w), 2):
        SCRATCH[_w[_i]] = ("sbuf", [128, int(_w[_i + 1])], _d)
for _d, _l in (("smi", "pi 8 tvi 64 tvj 64 uli 8"), ("smu", "chu 8 ul 8 pmu 16 psu 64 ivu 64 rku 24 lr 24 lja 16 ljb 16"),
               ("smf", "pf 24 cst 24 kt 8 z16 16 vb 24 xt1 8 xt2 24 lf 24 lg 24 lc 24 rk 24 ivf 16 a3 24 ra 24 ends 64")):
    _w, _at = _l.split(), 0
    for _i in range(0, len(_w), 2):
        PART[_w[_i]] = (_d, _at)
        _at += int(_w[_i + 1])
for _r in range(3):
    for _n in ("qs", "ql"):
        SCRATCH["%s%d" % (_n, _r)] = ("sbuf", [128, H], COD)
    for _n in ("ss", "sl"):
        SCRATCH["%s%d" % (_n, _r)] = ("sbuf", [128, H], PLN)
for _b in range(8):
    SCRATCH["p%d" % _b] = ("psum", [128, 512], F)
QSEM = {"vector": "nv", "scalar": "ns", "tensor": "nt", "g": "ng"}
SEMAPHORES = list(QSEM.values()) + ["d%d" % _i for _i in range(40)] + ["%s%d" % (_n, _r) for _r in range(3) for _n in ("ac", "as", "lc", "lp")]


def route(topo, src, dst):
    if topo.may_write(src, dst):
        return None
    able = [c for c in topo.cores_of(src) if c != src and topo.may_write(c, dst)]
    able.sort(key=lambda c: topo.die(c) != topo.die(src))
    return able[0], able[1]


def engines(topo, src, dst):
    return topo.engines(src, dst)[:8]


def send(g, T, topo, src, dst, v, frm, to, r):
    rid, pid = topo.addr(dst, src)
    e = engines(topo, src, dst)
    a, b = T[to][:], T[frm][:]
    if v == 0:
        a, b = a.bitcast(dt.uint8), b.bitcast(dt.uint8)
    g.remote_dma(a, b, T.sem[("ac%d", "as%d")[v] % r], T.sem[("lc%d", "lp%d")[v] % r], pid, rid, sum(1 << i for i in e))
    return len(e)


def relay_program(g, core, T, topo):
    n = len(T.cores)
    for r, d in enumerate(DIST):
        for i in range(n):
            src, dst = T.cores[i], T.cores[(i + d) % n]
            way = route(topo, src, dst)
            if way is None or core not in way:
                continue
            v = way.index(core)
            g.wait_ge(T.sem[("ac%d", "as%d")[v] % r], len(engines(topo, src, core)))
            land = ("ql%d", "sl%d")[v] % r
            k = send(g, T, topo, core, dst, v, land, land, r)
            g.wait_ge(T.sem[("lc%d", "lp%d")[v] % r], k)


def rank_program(g, core, T, topo):
    rank = T.rank_of(core)
    if rank is None:
        relay_program(g, core, T, topo)
        return
    n = len(T.cores)
    eng = {"vector": g.vector, "scalar": g.scalar, "tensor": g.tensor, "g": g, "sync": g.sync}
    count = {q: 0 for q in QSEM}
    known = {q: {} for q in eng}
    hist, ndma, total = {}, [0], {}

    def meets(a, b):
        if a[0] >= b[1] or b[0] >= a[1] or a[2] >= b[3] or b[2] >= a[3]:
            return False
        return not (a[4] == b[4] and a[4] > 1 and (a[2] - b[2]) % a[4])

    def bank(name):
        return len(name) == 2 and name[0] == "p" and name[1].isdigit()

    def A(name, c0, c1, step=1, p0=0, p1=128):
        if name in PART:
            name, k = PART[name]
            c0, c1 = c0 + k, c1 + k
        return {"ap": T[name][p0:p1, c0:c1:step] if step > 1 else T[name][p0:p1, c0:c1], "reg": [(name, (0, 128, 0, 512, 1) if bank(name) else (p0, p1, c0, c1, step))], "off": []}

    def W(name, c0, c1, kind):
        return {"ap": T[name][:, c0:c1].bitcast(kind), "reg": [(name, (0, 128, c0, c1, 1))], "off": []}

    def I(w, o):
        return {"ap": w["ap"].indirect(o["ap"]), "reg": w["reg"], "off": o["reg"]}

    def need(q, reads, writes, goes_on=False):
        want = {}
        for k, views in ((0, reads), (1, writes)):
            for v in views:
                for kk, name, reg in [(k, a, b) for a, b in v["reg"]] + [(0, a, b) for a, b in v["off"]]:
                    for (oreg, ok, oq, sem, val, snap) in hist.get(name, []):
                        if not meets(reg, oreg) or not (kk or ok or bank(name) and oq != q) or goes_on and kk and oq == q:
                            continue
                        if want.get(sem, (0,))[0] < val:
                            want[sem] = (val, snap)
        for sem in sorted(want):
            val, snap = want[sem]
            if known[q].get(sem, 0) >= val:
                continue
            eng[q].wait_ge(T.sem[sem], val)
            for s, x in snap.items():
                known[q][s] = max(known[q].get(s, 0), x)
            known[q][sem] = val

    def note(q, reads, writes, sem, val, snap):
        total[sem] = max(total.get(sem, 0), val)
        for k, views in ((0, reads), (1, writes)):
            for v in views:
                for kk, name, reg in [(k, a, b) for a, b in v["reg"]] + [(0, a, b) for a, b in v["off"]]:
                    h = hist.setdefault(name, [])
                    if kk:
                        h[:] = [e for e in h if not (e[0][0] >= reg[0] and e[0][1] <= reg[1] and e[0][2] >= reg[2] and e[0][3] <= reg[3] and (reg[4] == 1 or reg[4] == e[0][4] and (reg[2] - e[0][2]) % reg[4] == 0))]
                    h.append((reg, kk, q, sem, val, snap))

    def emit(q, call, reads, writes, goes_on=False):
        need(q, reads, writes, goes_on)
        count[q] += 1
        snap = dict(known[q])
        call().then_inc(T.sem[QSEM[q]], 1)
        note(q, reads, writes, QSEM[q], count[q], snap)

    def dma(q, out, in_, reads, writes):
        need(q, reads, writes)
        sem = "d%d" % ndma[0]
        ndma[0] += 1
        eng[q].dma_start(out, in_).then_inc(T.sem[sem], 16)
        note("dma", reads, writes, sem, 16, dict(known[q]))

    def copy(out, in_):
        emit("vector", lambda: g.vector.tensor_copy(out["ap"], in_["ap"]), [in_], [out])

    def ts(out, in_, s1, s2, o0, *o1):
        a = [s["ap"] if isinstance(s, dict) else s for s in (s1, s2)]
        emit("vector", lambda: g.vector.tensor_scalar(out["ap"], in_["ap"], a[0], a[1], o0, *o1), [in_] + [s for s in (s1, s2) if isinstance(s, dict)], [out])

    def tt(out, a, b, o):
        emit("vector", lambda: g.vector.tensor_tensor(out["ap"], a["ap"], b["ap"], o), [a, b], [out])

    def add_runs(s, m, c0, w):
        sv, rs, mv = A(s, c0, c0 + w), A("rst", 0, w), A(m, c0, c0 + w)
        emit("vector", lambda: g.vector.tensor_tensor_scan(sv["ap"], rs["ap"], mv["ap"], 0.0, Op.mult, Op.add), [rs, mv], [sv])

    def fill(v, c):
        emit("vector", lambda: g.vector.memset(v["ap"], c), [], [v])

    def quant(q, s, c0, c1, src):
        oq, os_ = A(q, c0, c1), A(s, c0, c1)
        emit("vector", lambda: g.vector.quantize_mx(oq["ap"], os_["ap"], src["ap"]), [src], [oq, os_])

    def act(out, in_, f=AF.Copy, accum=None, scale=None):
        k = {} if scale is None else {"scale": scale}
        if accum:
            k["accum_out"] = accum["ap"]
        emit("scalar", lambda: g.scalar.activation(out["ap"], in_["ap"], f, **k), [in_], [out] + ([accum] if accum else []))

    def mm(b, w, sw, w0, x, sx, x0, x1, start=True, stop=True):
        o, v = A(b, 0, x1 - x0), [A(w, w0, w0 + 128), A(sw, w0, w0 + 128), A(x, x0, x1), A(sx, x0, x1)]
        emit("tensor", lambda: g.tensor.matmul_mx(o["ap"], v[0]["ap"], v[1]["ap"], v[2]["ap"], v[3]["ap"], start, stop), v, [o], not start)

    def iota(v, pattern, base, cm, small=True):
        k = {"allow_small_or_imprecise_dtypes": True} if small else {}
        emit("g", lambda: g.iota(v["ap"], pattern, base, cm, **k), [], [v])

    def turn32(o, i_):
        emit("vector", lambda: g.vector.transpose(o["ap"], i_["ap"]), [i_], [o])

    def exchange(x, a, b):
        def quarters():
            for q in range(4):
                (act if q % 2 else copy)(A(x, 64, 128, 1, 32 * q, 32 * q + 32), A(x, 0, 64, 1, 32 * (q ^ 1), 32 * (q ^ 1) + 32))

        def second():
            copy(A(b, 0, 16), A(a, 16, 32))
            act(A(b, 16, 32), A(a, 0, 16))

        def halves():
            copy(A(x, 128, 256, 1, 0, 64), A(x, 0, 128, 1, 64, 128))
            act(A(x, 128, 256, 1, 64, 128), A(x, 0, 128, 1, 0, 64))
        return [lambda: turn32(A(a, 0, 32), A(x, 0, 32)), second, lambda: turn32(A(x, 32, 64), A(b, 0, 32)), quarters, halves]

    LAG, CMP = 0.1, 0.25

    def merge(side, gap, *strands):
        todo = [[(f, c, w) for items, c, w in s for f in items] for s in strands]
        left = [sum(c + w for _, c, w in s) for s in todo]
        free, now, due = [0.0] * len(todo), 0.0, 0.0
        side = list(side)
        while any(todo):
            while side and due <= now:
                side.pop(0)()
                due += gap
            live = [k for k in range(len(todo)) if todo[k]]
            able = [k for k in live if free[k] <= now]
            if not able:
                now = min(free[k] for k in live)
                continue
            k = max(able, key=lambda j: left[j])
            f, c, w = todo[k].pop(0)
            f()
            now += c
            free[k] = now + w
            left[k] -= c + w
        for f in side:
            f()

    def load(q, v, src):
        dma(q, v["ap"], src, [], [v])
    load("sync", A("xt", 0, 1280), T.x[:])
    load("scalar", A("ut", 0, 512), T.u[:])
    for i in range(8):
        load(("sync", "scalar")[i % 2], A("ch4", 0, 4, 1, 16 * i, 16 * i + 16), T.ch[:])
    load("sync", W("qw", 0, 512, dt.uint8), T.wc[:])
    load("sync", A("sw", 0, 512), T.ws[:])
    load("sync", A("vt", 0, 512), T.v[:])

    def pf(i):
        return A("pf", i, i + 1)

    def pi(i):
        return A("pi", i, i + 1)
    iota(pi(0), [[0, 1]], 0, 1, False)
    iota(A("uli", 0, 8), [[16, 8]], 0, 0, False)
    iota(A("tvi", 0, 64), [[1, 4], [4, 16]], 0, 0, False)
    iota(A("io16", 0, 512), [[0, 32], [1, 16]], 0, 0)
    fill(A("one", 0, 128), 1.0)
    fill(A("zz", 0, 4680), 0.0)

    def pattern(z, pat, base):
        o, i_ = A("zz", 520 * z + 3, 520 * z + 515, 4), A("one", 0, 128)
        emit("g", lambda: g.affine_select(o["ap"], i_["ap"], pat, Op.is_equal, 0.0, base, 1), [i_], [o])
    iota(A("iog", 0, 512), [[1, 8], [0, 64]], 0, 0)
    iota(A("cv", 0, C), [[1, C]], 0, 0)
    iota(A("cst", 0, 20), [[-16, 20]], 319, 0)
    for h in range(8):
        pattern(h, [[0, 8], [-1, 16]], -16 * h)
    pattern(8, [[-1, 128]], 0)
    iota(A("vb", 0, 8), [[0, 4], [1, 2]], 0, 0)
    iota(A("vb", 8, 16), [[0, 2], [1, 2], [0, 2]], 0, 0)
    iota(A("vb", 16, 24), [[1, 2], [0, 4]], 0, 0)
    iota(A("kt", 0, 4), [[1, 4]], 0, 0)
    iota(A("hw", 0, 2560), [[1, 8], [0, 320]], 0, 0)

    ts(pi(1), pi(0), 15, None, Op.bitwise_and)
    ts(pi(2), pi(0), 4, None, Op.logical_shift_right)
    copy(pf(8), pi(0))
    copy(A("ul", 0, 8), A("uli", 0, 8))
    ts(A("tvj", 0, 64), A("tvi", 0, 64), 7, None, Op.bitwise_and)
    ts(pi(3), pi(1), 1, None, Op.logical_shift_right)
    copy(pf(0), pi(1))
    copy(pf(1), pi(2))
    for i, w in ((1, 4.0), (2, 2.0), (3, 1.0)):
        ts(pf(9 + i), pf(8), float(i), w, Op.is_equal, Op.mult)
    ts(pf(2), pi(3), 8.0, None, Op.mult)
    ts(A("tv", 0, 64), A("tvj", 0, 64), 4096.0, None, Op.mult)
    ts(A("msk", 0, 512), A("io16", 0, 512), pf(0), None, Op.is_equal)
    tt(pf(13), pf(10), pf(11), Op.add)
    ts(A("rst", 0, 512), A("io16", 0, 512), 0.0, None, Op.not_equal)
    tt(pf(14), pf(13), pf(12), Op.add)
    fill(A("kk", 0, 1536), 0.0)
    quant("qu", "su", 0, 128, A("ut", 0, 512))
    quant("qx", "sx", 0, C, A("xt", 0, 1280))
    WID, MC = [128, 128, 192, 256, 320], [0, 128, 256, 448, 704]

    tabs = [lambda: ts(A("chu", 0, 4), A("ch4", 0, 4), pf(2), None, Op.add), lambda: copy(I(A("tab", 0, 64), A("chu", 0, 4)), A("tv", 0, 64))]

    def lists(lst, w, k):
        c = w // 16
        return lambda: ts(A(lst, c * k, c * k + c), A("ts", 15, w, 16), 1.0 / 4096, 8.0 * k, Op.mult, Op.add)
    for (lst, w, b0) in (("l2", 64, 0), ("l3", 512, 64)):
        tabs += [lambda w=w, b0=b0: tt(A("tm", 0, w), A("tab", b0, b0 + w), A("msk", 0, w), Op.mult), lambda w=w: add_runs("ts", "tm", 0, w)]
        tabs += [lists(lst, w, k) for k in range(8)]
        if w == 64:
            tabs += [lambda: copy(A("tab", 64, 576), I(A("tab", 0, 64), A("l2", 0, 32)))]
    tabs += [lambda: act(A("tab", 576, TEND), I(A("tab", 0, 64), A("l3", 0, 256)))]

    copy(W("qur", 0, 128, dt.uint32), I(W("qu", 0, 128, dt.uint32), A("ul", 0, 8)))
    copy(A("sur", 0, 128), I(A("su", 0, 128), A("ul", 0, 8)))
    for m in range(3):
        for d, s in [(0, 1.0)] + [(e + 1, -1.0) for e in range(m)]:
            ts(A("kk", 512 * d + m, 512 * d + 512, 4), A("one", 0, 128), pf(14), s * 8.0 ** (m + 1), Op.mult, Op.mult)
    ts(A("kk", 1536, 2048), A("iog", 0, 512), pf(1), -1.0, Op.is_equal, Op.mult)
    fill(A("btb", 0, 512), 0.0)
    fill(A("bta", 0, 512), 0.0)
    for j in range(4):
        quant("ck", "sk", 128 * j, 128 * j + 128, A("kk", 512 * j, 512 * j + 512))
    ts(A("cap", 0, C), A("io16", 0, C), pf(0), 2e29, Op.is_lt, Op.mult)
    fill(A("z16", 0, 16), 0.0)
    ts(A("cap", 0, C), A("cap", 0, C), -1e29, None, Op.add)
    for j in range(4, -1, -1):
        fill(A("m%d" % j, 256 * j, 4 * WID[j]), 0.0)

    late = [lambda: ts(pf(3), pf(1), 320.0, None, Op.mult), lambda: ts(pf(4), pf(1), 4096.0, None, Op.mult), lambda: ts(pf(5), pf(1), 4096.0, 4096.0, Op.mult, Op.add),
            lambda: ts(pf(7), pf(1), -114688.0, -114688.0, Op.mult, Op.add)]
    late += [lambda b=b: ts(pi(4 + b), pi(0), 4 + b, None, Op.logical_shift_right) for b in range(3)]
    late += [lambda: ts(A("cv", 0, C), A("cv", 0, C), pf(3), None, Op.add), lambda: fill(A("fca", 0, 144), 0.0)]
    late += [lambda b=b: ts(pi(4 + b), pi(4 + b), 1, None, Op.bitwise_and) for b in range(3)]
    late += [lambda: ts(A("cst", 0, 20), A("cst", 0, 20), pf(0), None, Op.subtract), lambda: fill(A("xa", 0, 32), 0.0)]
    late += [lambda b=b: copy(pf(16 + b), pi(4 + b)) for b in range(3)]
    late += [lambda: ts(A("kt", 0, 4), A("kt", 0, 4), pf(7), None, Op.add)]
    late += [lambda b=b: ts(A("xt2", 8 * b, 8 * b + 8), A("vb", 8 * b, 8 * b + 8), pf(16 + b), 32.0 * 2 ** b, Op.not_equal, Op.mult) for b in range(3)]
    late += [lambda: fill(A("xb", 0, 288), 0.0), lambda: tt(A("xt2", 0, 8), A("xt2", 0, 8), A("xt2", 8, 16), Op.add), lambda: tt(A("xt2", 0, 8), A("xt2", 0, 8), A("xt2", 16, 24), Op.add),
             lambda: ts(A("xt1", 0, 8), A("xt2", 0, 8), pf(0), None, Op.add)]

    turn = [0]

    def begin(c0, c1, bt, qb, sb, i9, off, bk, starts):
        mm("p1", "qu", "su", 0, "qx", "sx", c0, c1)
        mm(bk, "qur", "sur", 0, "qx", "sx", c0, c1)
        w = c1 - c0
        for m in range(3):
            k = len(range(m, w, 3))
            ts(A(bt, m, m + 4 * k - 3, 4), A("p1", m, w, 3), 0.0, None, Op.is_gt)
        tt(A("sm", c0, c1), A(bk, 0, w), A("msk", 0, w), Op.mult)
        quant(qb, sb, 0, 128, A(bt, 0, 512))
        for j, b in enumerate(("p2", "p3", "p4")):
            mm(b, "ck", "sk", 128 * j, qb, sb, 0, 128)
            act(A(i9, 128 * j, 128 * j + 128), A(b, 0, 128))
        add_runs("sc", "sm", c0, w)
        tt(A("sd", c0, c1), A(bk, 0, w), A("cap", 0, w), Op.min)
        for b in starts:
            ts(A(off, 16 * b, 16 * b + 16), A("z16", 0, 16), A(i9, b, b + 1), pf(1), Op.add, Op.add)

    def step(i9, off, b):
        return lambda: ts(A(off, 16 * b + 16, 16 * b + 32), I(A("tab", TB[2], TEND), A(off, 16 * b, 16 * b + 1)), 1.0 / 4096, A(i9, b + 1, b + 2), Op.mult, Op.add)

    def end(s):
        b = 16 * s + 15
        return lambda: ts(A("ends", 16 * s, 16 * s + 16), I(A("tab", TB[2], TEND), A("offb", 16 * b, 16 * b + 1)), 1.0 / 4096, None, Op.mult)

    def places(off, i9, k, w, fc, fm, fs, lj):
        a = [lambda: copy(A(fc, 2 * w, 2 * w + k), A(off, 0, 16 * k, 16))]
        a += [lambda d=d: tt(A(fc, w * d, w * d + k), A(i9, 128 * d + 128, 128 * d + 128 + k), A(fc, 2 * w, 2 * w + k), Op.add) for d in (0, 1)]
        a += [lambda: tt(A(fm, 0, 3 * w), A(fc, 0, 3 * w), A("msk", 0, 3 * w), Op.mult), lambda: add_runs(fs, fm, 0, 3 * w)]
        a += [lambda m=m: ts(A(lj, 4 * m, 4 * m + w // 16), A(fs, w * m + 15, w * m + w, 16), float(TB[m]), None, Op.add) for m in range(3)]
        return a

    def spread(first, c0, c1, banks):
        def one(h, b):
            def go():
                e = 128 * (4 * h + b)
                if first:
                    quant("ce", "se", e, e + 128, A("zz", 520 * h + 3 - b, 520 * h + 515 - b))
                bk = banks[turn[0] % len(banks)]
                turn[0] += 1
                mm(bk, "ce", "se", e, "qx", "sx", c0, c1)
                act(A("win", 1280 * h + 4 * c0 + b, 1280 * h + 4 * c1, 4), A(bk, 0, c1 - c0))
            return go
        return [one(h, b) for h in range(8) for b in range(4)]

    def ge(k, src, lo, hi, base):
        ts(A("m%d" % (k // 4), 4 * lo + k % 4, 4 * hi, 4), A(src, lo - base, hi - base), A("sc", 16 * k + 15, 16 * k + 16), None, Op.is_ge)

    def add_up(k, lo, hi, to):
        act(A("j%d" % (k % 2), lo, hi), A("m%d" % (k // 4), 4 * lo + k % 4, 4 * hi, 4), AF.Copy, accum=A(to, k, k + 1))

    def compare_b(k):
        def go():
            if k > 8:
                ge(k, "p5", H, 16 * k, H)
            ge(k, "sd", 16 * k, 16 * k + 16, 0)
            add_up(k, H, 16 * k + 16, "lg")
            if k % 4 == 0 and k > 8:
                j = k // 4
                quant("qm", "smm", MC[j] + H, MC[j] + WID[j], A("m%d" % j, 4 * H, 4 * WID[j]))
        return go

    def compare_a(k):
        def go():
            j, hi = k // 4, min(H, 16 * k)
            if k:
                ge(k, "p0", 0, hi, 0)
            if k < 8:
                ge(k, "sd", 16 * k, 16 * k + 16, 0)
                hi += 16
            add_up(k, 0, hi, "lf")
            if k % 4 == 0:
                w = H if j > 2 else WID[j]
                quant("qm", "smm", MC[j], MC[j] + w, A("m%d" % j, 0, 4 * w))
                mm("p1", "ck", "sk", 384, "qm", "smm", MC[j], MC[j] + WID[j], j == 4, j == 0)
        return go

    def begin_b():
        begin(H, C, "btb", "qbb", "sbb", "i9b", "offb", "p5", (0, 16, 32, 48))

    def begin_a():
        begin(0, H, "bta", "qba", "sba", "i9a", "offa", "p0", (0,))
    cmp_b, cmp_a = [compare_b(k) for k in range(19, 7, -1)], [compare_a(k) for k in range(19, -1, -1)]
    chain_b = [step("i9b", "offb", 16 * s + b) for b in range(15) for s in range(4)] + [end(s) for s in range(4)]
    tail_b = places("offb", "i9b", 64, 64, "fcb", "fmb", "fsb", "ljb")
    tail_b += [lambda m=m: copy(A("ib", m, 192, 3), I(A("tab", 0, TEND), A("ljb", 4 * m, 4 * m + 4))) for m in range(3)]
    tail_b += [lambda: tt(A("im", 0, 192), A("ib", 0, 192), A("msk", 0, 192), Op.mult), lambda: act(A("xb", 4, 29, 8), A("ends", 0, 64, 16)), lambda: add_runs("is1", "im", 0, 192)]
    tail_b += [lambda s=s: (act if s % 2 else copy)(A("xb", 8 * s, 8 * s + 3), A("is1", 48 * s + 15, 48 * s + 48, 16)) for s in range(4)]
    tail_b += exchange("xb", "u1", "u2")
    chain_a = [step("i9a", "offa", b) for b in range(42)]
    chain_a += [lambda: ts(A("pmu", 0, 16), I(A("tab", TB[1], TB[2]), A("offa", 16 * 42, 16 * 42 + 1)), 1.0 / 4096, None, Op.mult)]
    chain_a += places("offa", "i9a", 43, 48, "fca", "fma", "fsa", "lja")
    way_b = []
    for s in range(4):
        at = A("ivu", 16 * s - 12, 16 * s - 11) if s else A("pmu", 0, 1)
        way_b += [lambda s=s, at=at: copy(A("psu", 16 * s, 16 * s + 16), I(A("xt1", 0, 8), at)),
                  lambda s=s: copy(A("ivu", 16 * s, 16 * s + 16), I(A("xb", 8 * s, 8 * s + 248), A("psu", 16 * s, 16 * s + 1)))]
    rank_ = [lambda: tt(A("zm", 0, C), A("p1", 0, C), A("msk", 0, C), Op.mult), lambda: tt(A("lc", 8, 20), A("lf", 8, 20), A("lg", 8, 20), Op.add), lambda: add_runs("zs", "zm", 0, C),
             lambda: copy(A("lc", 0, 8), A("lf", 0, 8)), lambda: tt(A("ra", 0, 20), A("lc", 0, 20), A("cst", 0, 20), Op.add),
             lambda: tt(A("rk", 0, 20), A("zs", 15, C, 16), A("ra", 0, 20), Op.add), lambda: copy(A("rku", 0, 20), A("rk", 0, 20)), lambda: copy(I(A("ow", 0, C), A("rku", 0, 20)), A("cv", 0, C)),
             lambda: tt(A("lm", H, C), A("ow", H, C), A("msk", 0, C - H), Op.mult)]

    def finish():
        parts = [lambda m=m: tt(A("la", m, 144, 3), I(A("tab", 0, TEND), A("lja", 4 * m, 4 * m + 3)), A("ow", m, 144, 3), Op.add) for m in range(3)]
        parts += [lambda: tt(A("lm", 0, H), A("la", 0, H), A("msk", 0, H), Op.mult), lambda: add_runs("ls", "lm", 0, C), lambda: act(A("xa", 0, 8), A("ls", 15, H, 16))]
        merge([], 1.0, [(parts, 0.25, LAG)], [(way_b, 0.07, LAG)])
        for s in range(4):
            copy(A("ivf", 3 * s, 3 * s + 3), A("ivu", 16 * s, 16 * s + 3))
        tt(A("xa", 8, 20), A("ls", H + 15, C, 16), A("ivf", 0, 12), Op.add)
        for f in exchange("xa", "t1", "t2"):
            f()
        ts(A("cl", 0, 256), A("xa", 0, 256), pf(4), pf(5), Op.max, Op.min)
        tt(A("a1", 0, 128), A("cl", 0, 128), A("cl", 128, 256), Op.add)
        tt(A("a2", 0, 64), A("a1", 0, 64), A("a1", 64, 128), Op.add)
        tt(A("a3", 0, 20), A("a2", 0, 20), A("a2", 32, 52), Op.add)
        for t in (2, 0, 3, 1):
            ts(A("lt", 20 * t, 20 * t + 20), A("a3", 0, 20), 4.0, A("kt", t, t + 1), Op.mult, Op.add)

    def gather(c0, c1):
        for t in (2, 0, 3, 1):
            (copy if t < 2 else act)(A("tt", 4 * c0 + t, 4 * c1, 4), I(A("win", 0, 10240), A("lt", 20 * t + c0 // 16, 20 * t + c1 // 16)))

    def store(c0, c1):
        q = W("qx", c0, c1, dt.uint8)
        dma("sync", T.oc[:, 4 * c0:4 * c1], q["ap"], [q], [])
        for k in range(4):
            s = A("sx", c0, c1, 1, 32 * k, 32 * k + 4)
            dma("sync", T.osc[4 * k:4 * k + 4, c0:c1], s["ap"], [s], [])
        mm("p1", "qv", "sv", 0, "qx", "sx", c0, c1)
        y = A("yt", c0, c1)
        act(y, A("p1", 0, c1 - c0))
        dma("scalar", T.y[:, c0:c1], y["ap"], [y], [])

    begin_b()
    begin_a()
    wide = spread(True, 0, C, ("p6", "p7", "p2", "p3", "p4"))
    pause = ([lambda: None], 0.0, 5.0)
    merge(wide[:10], 0.7, [(tabs, 0.07, LAG)], [(late, 0.06, 0.0)], [(cmp_b, CMP, 0.0)])
    merge(wide[10:], 0.4, [(cmp_a, CMP, 0.0), (rank_, 0.3, LAG)], [pause, (chain_a, 0.07, LAG)], [pause, (chain_b, 0.07, 0.0), (tail_b, 0.1, LAG)])
    rest_b, wide = [], []
    for r, d in enumerate(DIST):
        if r:
            begin_a()
            merge(wide + spread(False, 0, H, ("p6", "p7", "p2", "p3", "p4")), 0.2, [(rest_b, CMP, 0.0), (cmp_a, CMP, 0.0), (rank_, 0.3, LAG)], [(chain_a, 0.07, LAG)], [(tail_b, 0.1, LAG)])
        finish()
        gather(0, H)
        mine, land = ("qs%d" % r, "ss%d" % r), ("ql%d" % r, "sl%d" % r)
        quant(mine[0], mine[1], 0, H, A("tt", 0, 4 * H))
        dst, src = T.cores[(rank + d) % n], T.cores[(rank - d) % n]
        way, last = route(topo, core, dst), route(topo, src, core)
        for v in (0, 1):
            i_ = A(mine[v], 0, H)
            need("g", [i_], [])
            k = send(g, T, topo, core, way[v] if way else dst, v, mine[v], land[v], r)
            note("net", [i_], [], ("lc%d", "lp%d")[v] % r, k, dict(known["g"]))
        gather(H, C)
        quant("qx", "sx", H, C, A("tt", 4 * H, 4 * C))
        if r < 2:
            begin_b()
            wide = spread(False, H, C, ("p6", "p7", "p2", "p3", "p4"))
            merge(wide[:28], 0.2, [(cmp_b[:9], CMP, 0.0)], [(chain_b, 0.07, 0.02)])
            rest_b, wide = cmp_b[9:], wide[28:]
        else:
            ts(A("rk", 0, 20), A("a3", 0, 20), 4.0, A("kt", 0, 1), Op.mult, Op.add)
            ts(A("lr", 0, 20), A("rk", 0, 20), 0.25, None, Op.mult)
            copy(A("rwt", 0, C), I(A("hw", 0, 2560), A("lr", 0, 20)))
            i_ = A("rwt", 0, C)
            dma("sync", T.rw[:], T["rwt"][0:128:16, 0:C], [i_], [])
            store(H, C)
        if r == 0:
            for b in range(4):
                quant("cei", "sei", 128 * b, 128 * b + 128, A("zz", 4163 - b, 4675 - b))
            quant("qv", "sv", 0, 128, A("vt", 0, 512))
        for v in (0, 1):
            note("net", [], [A(land[v], 0, H)], ("ac%d", "as%d")[v] % r, len(engines(topo, last[v] if last else src, core)), {})
        pw, pe = ("p2", "p3", "p4", "p0"), ("p6", "p7", "p1", "p6")
        for b in range(4):
            mm(pw[b], "qw", "sw", 128 * b, land[0], land[1], 0, H)
            mm(pe[b], "cei", "sei", 128 * b, land[0], land[1], 0, H)
            act(A("rl", 128 * b, 128 * b + 128), A(pw[b], 0, H), AF.Relu, scale=0.03125)
            tt(A("xn", b, 512, 4), A("rl", 128 * b, 128 * b + 128), A(pe[b], 0, H), Op.add)
        quant("qx", "sx", 0, H, A("xn", 0, 512))
    store(0, H)
    for sem in sorted(total):
        if known["g"].get(sem, 0) < total[sem]:
            g.wait_ge(T.sem[sem], total[sem])
